import numpy as np
import ml_dtypes


def mxq(x, axis, fmt="e4m3"):
    dtype, down = {"e4m3": (ml_dtypes.float8_e4m3fn, 7), "e5m2": (ml_dtypes.float8_e5m2, 14)}[fmt]
    v = np.moveaxis(np.asarray(x, np.float32).astype(ml_dtypes.bfloat16).astype(np.float64), axis, -1)
    blocks = v.reshape(v.shape[:-1] + (-1, 32))
    amax = np.abs(blocks).max(-1, keepdims=True)
    byte = np.maximum(np.where(amax > 0, np.frexp(amax)[1] - 1 + 127, 0) - down, 1)
    scale = np.exp2(byte - 127.0)
    codes = (blocks / scale).astype(np.float32).astype(dtype).astype(np.float64)
    return np.moveaxis((codes * scale).reshape(v.shape), -1, axis)


WIDE = False


def mx_kscale(k):
    if not WIDE:
        return np.ones(k)
    levels = np.array([10, -10, 5, -5, 0])
    if k % 512:
        return np.exp2(np.random.permutation(np.resize(levels, k // 32))).repeat(32)
    a = np.empty((k // 512, 16))
    for p in range(k // 512):
        a[p, :8] = np.random.permutation(np.resize(levels, 8))
        for g in range(8):
            far = levels[np.abs(levels - a[p, g]) >= 10]
            a[p, g + 8] = far[np.random.randint(len(far))]
    return np.exp2(a.ravel()).repeat(32)


BF16 = ml_dtypes.bfloat16


def bf(x):
    return np.asarray(x, np.float32).astype(BF16)


def f64(x):
    return np.asarray(x).astype(np.float64)

def planes(Y):
    n, m = Y.shape
    b = f64(bf(Y)).reshape(n // 32, 32, m)
    amax = np.abs(b).max(1)
    byte = np.clip(np.where(amax > 0, np.frexp(amax)[1] - 1 + 127 - 7, 1), 1, 254)
    codes = (b * np.exp2(127.0 - byte)[:, None, :]).reshape(n, m).astype(np.float32).astype(ml_dtypes.float8_e4m3fn).view(np.uint8)
    words = codes.reshape(n // 512, 128, 4, m).transpose(0, 1, 3, 2)
    return np.ascontiguousarray(words), np.ascontiguousarray(byte.astype(np.uint8).reshape(n // 512, 16, m))


N, L, K = 1024, 1024, 512


def linear_mixture(a, ef, psi, rho):
    return rho[None, :] * (mxq(a * psi[None, :], 1, "e4m3") @ mxq(ef, 0, "e4m3"))


def smooth_l1_grad(a):
    return 0.3 * a / np.sqrt(a * a + 0.01)


def setup_inputs():
    s, t = mx_kscale(L), mx_kscale(K)
    return {
        "y": bf(np.random.standard_normal((N, K)) * 0.5),
        "a": bf(np.random.standard_normal((N, L)) * 0.5),
        "e": bf(np.random.standard_normal((L, K)) / np.sqrt(L) / s[:, None] / t[None, :]),
        "psi": bf((1.0 + 0.1 * np.random.standard_normal(L)) * s),
        "rho": bf((1.0 + 0.1 * np.random.standard_normal(K)) * t),
        "b": bf(np.random.standard_normal(N) * 0.5),
    }


def core(y, a, e, psi, rho, b):
    yf, af, ef, psif, rhof = f64(y), f64(a), f64(e), f64(psi), f64(rho)
    bn = f64(b)[:, None]
    m = linear_mixture(af, ef, psif, rhof)
    p = m + bn * (m * m)
    q = (p - yf) * (1.0 + 2.0 * bn * m) * rhof[None, :]
    h = mxq(q, 1, "e4m3") @ mxq(ef, 1, "e4m3").T
    return psif[None, :] * h + smooth_l1_grad(af)


def reference(y, a, e, psi, rho, b):
    R_out = core(y, a, e, psi, rho, b)
    words, scales = planes(R_out.T)
    return R_out, words, scales

@@ -1,0 +1,477 @@
+from contextlib import ExitStack
+
+import concourse.mybir as mybir
+from concourse.masks import make_identity
+
+N, L, K = 1024, 1024, 512
+FLOPS = 2 * 2 * N * L * K
+
+F32 = mybir.dt.float32
+BF16 = mybir.dt.bfloat16
+U32 = mybir.dt.uint32
+I32 = mybir.dt.int32
+U8 = mybir.dt.uint8
+X4 = mybir.dt.float8_e4m3fn_x4
+ACT = mybir.ActivationFunctionType
+ALU = mybir.AluOpType
+
+P = 128
+G = L // 512
+C = 256
+NC = N // C
+NB = C // P
+
+
+def tile_polynomialpostnonlinearlibraryunmixinggr_x1_kernel(
+    tc, y, a, e, psi, rho, b, out_0, out_1, out_2
+):
+    nc = tc.nc
+    V, S, T = nc.vector, nc.scalar, nc.tensor
+    with ExitStack() as ctx:
+        keep = ctx.enter_context(tc.tile_pool(name="keep", bufs=1))
+        work = ctx.enter_context(tc.tile_pool(name="work", bufs=2))
+        psum = ctx.enter_context(tc.psum_pool(name="psum", bufs=2))
+
+        e_raw, a_raw, y_raw = [], [], []
+        for g in range(G):
+            e_raw.append(keep.tile([P, 4, K], BF16, name="e_raw%d" % g))
+        for c in range(NC):
+            a_raw.append(keep.tile([P, NB, L], BF16, name="a_raw%d" % c))
+            y_raw.append(keep.tile([P, NB, K], BF16, name="y_raw%d" % c))
+        b_col = keep.tile([P, 8], BF16, name="b_col")
+        psi4 = keep.tile([P, G, 4], BF16, name="psi4")
+        rho4 = keep.tile([P, 4], BF16, name="rho4")
+
+        ident = keep.tile([P, P], F32, name="ident")
+        ident_bf = keep.tile([P, P], BF16, name="ident_bf")
+        make_identity(nc, ident_bf[:])
+        make_identity(nc, ident[:])
+
+        def load_e(g):
+            nc.sync.dma_start(
+                out=e_raw[g][:], in_=e[512 * g : 512 * g + 512, :].rearrange("(p j) k -> p j k", j=4)
+            )
+
+        def load_a(c):
+            nc.sync.dma_start(
+                out=a_raw[c][:], in_=a[C * c : C * c + C, :].rearrange("(r p) l -> p r l", p=P)
+            )
+
+        def load_y(c):
+            nc.sync.dma_start(
+                out=y_raw[c][:], in_=y[C * c : C * c + C, :].rearrange("(r p) k -> p r k", p=P)
+            )
+
+        warm = keep.tile([P, 1], F32, name="warm")
+        rho_f = keep.tile([P, 4], F32, name="rho_f")
+        rho_2 = keep.tile([P, 4], F32, name="rho_2")
+        rho_h = keep.tile([P, 4], F32, name="rho_h")
+        b_all = keep.tile([P, N], BF16, name="b_all")
+        e1_codes = keep.tile([P, G, 512], U32, align_bytes=64, name="e1_codes")
+        e1_scales = keep.tile([P, G, 512], U8, align_bytes=64, name="e1_scales")
+        e2_codes = keep.tile([P, G, 512], U32, align_bytes=64, name="e2_codes")
+        e2_scales = keep.tile([P, G, 512], U8, align_bytes=64, name="e2_scales")
+        e1_in = [keep.tile([P, 2048], BF16, align_bytes=64, name="e1_in%d" % g) for g in range(G)]
+        e2_in = [keep.tile([P, 2048], BF16, align_bytes=64, name="e2_in%d" % g) for g in range(G)]
+        p_scales = keep.tile([P, G, N], U8, align_bytes=64, name="p_scales")
+
+        at, ap_in, ap_codes, ap_scales, sq, pen = {}, {}, {}, {}, {}, {}
+        yt, yr, m1, u2, xx, dd, q_in, q_codes, q_scales = {}, {}, {}, {}, {}, {}, {}, {}, {}
+        h2, res, p_in, o_ps, o_sb = {}, {}, {}, {}, {}
+
+        def b_spread():
+            bp = psum.tile([P, 8, P], BF16, tag="tp", name="bp")
+            for i in range(8):
+                T.transpose(bp[:, i, :], b_col[:, i : i + 1].to_broadcast([P, P]), ident_bf[:])
+            S.copy(
+                out=b_all[:].rearrange("x (p i) -> x p i", i=8),
+                in_=bp[:].rearrange("x i p -> x p i"),
+            )
+
+        def e1_slices(eng_copy, g, t0, t1):
+            eng_copy(
+                out=e1_in[g][:].rearrange("p (t m j) -> p t m j", t=4, j=4)[:, t0:t1],
+                in_=e_raw[g][:].rearrange("p j (m t) -> p t m j", t=4)[:, t0:t1],
+            )
+
+        def e1_quant(g):
+            V.quantize_mx(out=e1_codes[:, g, :].bitcast(X4), scales=e1_scales[:, g, :], in_=e1_in[g][:])
+
+        def e2_turn(g, h):
+            ep = psum.tile([P, 2, 2, P], F32, tag="tp", name="ep")
+            for i in range(2):
+                words = e_raw[g][:, 2 * h + i, :].bitcast(F32)
+                for u in range(2):
+                    T.transpose(ep[:, i, u, :], words[:, u:256:2], ident[:])
+            return ep
+
+        def e2_copy(g, h, ep):
+            S.copy(
+                out=e2_in[g][:].bitcast(F32).rearrange("p (i m u) -> p i m u", i=4, u=2)[:, 2 * h : 2 * h + 2],
+                in_=ep[:].rearrange("p i u m -> p i m u"),
+            )
+
+        def e2_quant(g):
+            V.quantize_mx(out=e2_codes[:, g, :].bitcast(X4), scales=e2_scales[:, g, :], in_=e2_in[g][:])
+
+        def a_turn(c, g):
+            t = psum.tile([P, 2, C], F32, tag="at", name="at")
+            at[c, g] = t
+            for r in range(NB):
+                words = a_raw[c][:, r, :].bitcast(F32)
+                for u in range(2):
+                    T.transpose(
+                        t[:, u, P * r : P * r + P], words[:, 256 * g + u : 256 * g + 256 : 2], ident[:]
+                    )
+
+        def a_mul(c, g):
+            t = work.tile([P, C, 4], BF16, align_bytes=64, tag="ap_in%d" % g, name="ap_in")
+            ap_in[c, g] = t
+            V.tensor_tensor(
+                out=t[:].rearrange("p n (u s) -> p n u s", u=2),
+                in0=at[c, g][:].bitcast(BF16).rearrange("p u (n s) -> p n u s", s=2),
+                in1=psi4[:, g, :].rearrange("p (o u s) -> p o u s", o=1, u=2).to_broadcast([P, C, 2, 2]),
+                op=ALU.mult,
+            )
+
+        def a_quant(c, g):
+            if g == 0:
+                ap_codes[c] = work.tile([P, G, C], U32, align_bytes=64, tag="ap_codes", name="ap_codes")
+                ap_scales[c] = work.tile([P, G, C], U8, align_bytes=64, tag="ap_scales", name="ap_scales")
+            V.quantize_mx(
+                out=ap_codes[c][:, g, :].bitcast(X4),
+                scales=ap_scales[c][:, g, :],
+                in_=ap_in[c, g][:].rearrange("p n t -> p (n t)"),
+            )
+
+        def flat(c, g):
+            return at[c, g][:].rearrange("p u n -> p (u n)").bitcast(BF16)
+
+        def a_square(c, g):
+            t = work.tile([P, 4 * C], F32, tag="sq%d" % g, name="sq")
+            sq[c, g] = t
+            S.activation(out=t[:], in_=flat(c, g), func=ACT.Square)
+
+        def a_rsqrt(c, g):
+            t = sq[c, g]
+            S.activation(
+                out=t[:], in_=t[:], func=ACT.Abs_reciprocal_sqrt, scale=1.0 / 0.09, bias=0.01 / 0.09
+            )
+
+        def a_pen(c, g):
+            t = work.tile([P, 2, C, 2], F32, tag="pen%d" % g, name="pen")
+            pen[c, g] = t
+            V.tensor_tensor(
+                out=t[:].rearrange("p u n s -> p (u n s)"), in0=flat(c, g), in1=sq[c, g][:], op=ALU.mult
+            )
+
+        def y_turn(c):
+            t = psum.tile([P, 2, C], F32, tag="tp", name="yt")
+            yt[c] = t
+            for r in range(NB):
+                words = y_raw[c][:, r, :].bitcast(F32)
+                for u in range(2):
+                    T.transpose(t[:, u, P * r : P * r + P], words[:, u:256:2], ident[:])
+
+        def y_gain(c):
+            t = work.tile([P, 4, C], F32, tag="yr", name="yr")
+            yr[c] = t
+            src = yt[c][:].bitcast(BF16).rearrange("p u (n s) -> p u s n", s=2)
+            for k in range(4):
+                S.activation(
+                    out=t[:, k, :], in_=src[:, k // 2, k % 2, :], func=ACT.Copy, scale=rho_f[:, k : k + 1]
+                )
+
+        def mm1(c):
+            for h in range(2):
+                t = psum.tile([P, 2, C], F32, tag="m1", name="m1")
+                m1[c, h] = t
+                for i in range(2):
+                    k = 2 * h + i
+                    for g in range(G):
+                        T.matmul_mx(
+                            out=t[:, i, :],
+                            lhsT=e1_codes[:, g, P * k : P * k + P].bitcast(X4),
+                            lhsT_scale=e1_scales[:, g, P * k : P * k + P],
+                            rhs=ap_codes[c][:, g, :].bitcast(X4),
+                            rhs_scale=ap_scales[c][:, g, :],
+                            start=(g == 0),
+                            stop=(g == G - 1),
+                        )
+
+        def q_u(c, k):
+            if k == 0:
+                u2[c] = work.tile([P, 4, C], F32, tag="u2", name="u2")
+            V.scalar_tensor_tensor(
+                out=u2[c][:, k, :],
+                in0=m1[c, k // 2][:, k % 2, :],
+                scalar=rho_2[:, k : k + 1],
+                in1=b_all[:, C * c : C * c + C],
+                op0=ALU.mult,
+                op1=ALU.mult,
+            )
+
+        def q_x(c, h):
+            if h == 0:
+                xx[c] = work.tile([P, 4, C], F32, tag="xx", name="xx")
+            V.scalar_tensor_tensor(
+                out=xx[c][:, 2 * h : 2 * h + 2, :],
+                in0=u2[c][:, 2 * h : 2 * h + 2, :],
+                scalar=2.0,
+                in1=m1[c, h][:],
+                op0=ALU.add,
+                op1=ALU.mult,
+            )
+
+        def q_d(c, k):
+            if k == 0:
+                dd[c] = work.tile([P, 4, C], F32, tag="dd", name="dd")
+            V.scalar_tensor_tensor(
+                out=dd[c][:, k, :],
+                in0=xx[c][:, k, :],
+                scalar=rho_h[:, k : k + 1],
+                in1=yr[c][:, k, :],
+                op0=ALU.mult,
+                op1=ALU.subtract,
+            )
+
+        def q_q(c):
+            t = work.tile([P, C, 4], BF16, align_bytes=64, tag="q_in", name="q_in")
+            q_in[c] = t
+            V.scalar_tensor_tensor(
+                out=t[:],
+                in0=u2[c][:].rearrange("p t n -> p n t"),
+                scalar=1.0,
+                in1=dd[c][:].rearrange("p t n -> p n t"),
+                op0=ALU.add,
+                op1=ALU.mult,
+            )
+
+        def q_quant(c):
+            q_codes[c] = work.tile([P, C], U32, align_bytes=64, tag="q_codes", name="q_codes")
+            q_scales[c] = work.tile([P, C], U8, align_bytes=64, tag="q_scales", name="q_scales")
+            V.quantize_mx(
+                out=q_codes[c][:].bitcast(X4),
+                scales=q_scales[c][:],
+                in_=q_in[c][:].rearrange("p n t -> p (n t)"),
+            )
+
+        def mm2(c, g, h):
+            t = psum.tile([P, 2, C], F32, tag="h2", name="h2")
+            h2[c, g, h] = t
+            for i in range(2):
+                k = 2 * h + i
+                T.matmul_mx(
+                    out=t[:, i, :],
+                    lhsT=e2_codes[:, g, P * k : P * k + P].bitcast(X4),
+                    lhsT_scale=e2_scales[:, g, P * k : P * k + P],
+                    rhs=q_codes[c][:].bitcast(X4),
+                    rhs_scale=q_scales[c][:],
+                    start=True,
+                    stop=True,
+                )
+
+        def r_add(c, g, h):
+            if h == 0:
+                res[c, g] = work.tile([P, 4, C], F32, tag="res%d" % g, name="res")
+            for i in range(2):
+                k = 2 * h + i
+                V.scalar_tensor_tensor(
+                    out=res[c, g][:, k, :],
+                    in0=h2[c, g, h][:, i, :],
+                    scalar=psi4[:, g, k : k + 1],
+                    in1=pen[c, g][:, k // 2, :, k % 2],
+                    op0=ALU.mult,
+                    op1=ALU.add,
+                )
+
+        def p_cast(copy, c, g):
+            t = work.tile([P, C, 4], BF16, align_bytes=64, tag="p_in%d" % g, name="p_in")
+            p_in[c, g] = t
+            copy(
+                out=t[:].rearrange("p (n i) t -> p n t i", i=4),
+                in_=res[c, g][:].rearrange("p t (n i) -> p n t i", i=4),
+            )
+
+        def p_quant(c, g):
+            codes = work.tile([P, C], U32, align_bytes=64, tag="p_codes%d" % g, name="p_codes")
+            V.quantize_mx(
+                out=codes[:].bitcast(X4),
+                scales=p_scales[:, g, C * c : C * c + C],
+                in_=p_in[c, g][:].rearrange("p n t -> p (n t)"),
+            )
+            nc.sync.dma_start(
+                out=out_1[g, :, C * c : C * c + C, :].rearrange("p m t -> p (m t)").bitcast(I32),
+                in_=codes[:].bitcast(I32),
+            )
+
+        def store_scales(n0, n1):
+            for s in range(4):
+                nc.sync.dma_start(
+                    out=out_2[:, 4 * s : 4 * s + 4, n0:n1].rearrange("g q m -> q g m").bitcast(I32),
+                    in_=p_scales[32 * s : 32 * s + 4, :, n0:n1].bitcast(I32),
+                )
+
+        def o_turn(c, g, nb):
+            t = psum.tile([P, 4, P], F32, tag="tp", name="ot")
+            o_ps[c, g, nb] = t
+            for k in range(4):
+                T.transpose(t[:, k, :], res[c, g][:, k, P * nb : P * nb + P], ident[:])
+
+        def o_copy(copy, c, g, nb):
+            if g == 0:
+                o_sb[c, nb] = work.tile([P, L], F32, tag="o_sb%d" % nb, name="o_sb")
+            copy(
+                out=o_sb[c, nb][:, 512 * g : 512 * g + 512].rearrange("n (p t) -> n p t", t=4),
+                in_=o_ps[c, g, nb][:].rearrange("n t p -> n p t"),
+            )
+
+        def o_store(c, nb, l0, l1):
+            n0 = C * c + P * nb
+            nc.sync.dma_start(out=out_0[n0 : n0 + P, l0:l1], in_=o_sb[c, nb][:, l0:l1])
+
+        with tc.manual_schedule():
+            S.dma_start(out=b_col[:], in_=b.rearrange("(p i) -> p i", i=8))
+            S.dma_start(out=rho4[:], in_=rho.rearrange("(p t) -> p t", t=4))
+            S.dma_start(out=psi4[:], in_=psi.rearrange("(g p t) -> p g t", g=G, t=4))
+            load_e(0)
+            load_a(0)
+            load_e(1)
+            load_y(0)
+            for c in range(1, NC):
+                load_a(c)
+                load_y(c)
+
+            V.memset(warm[:], 1.0)
+            S.activation(out=warm[:], in_=warm[:], func=ACT.Abs_reciprocal_sqrt)
+            V.tensor_copy(out=rho_f[:], in_=rho4[:])
+            V.tensor_scalar(out=rho_2[:], in0=rho4[:], scalar1=2.0, scalar2=None, op0=ALU.mult)
+            V.scalar_tensor_tensor(
+                out=rho_h[:], in0=rho4[:], scalar=0.5, in1=rho4[:], op0=ALU.mult, op1=ALU.mult
+            )
+
+            b_spread()
+            e1_slices(S.copy, 0, 3, 4)
+            e1_slices(V.tensor_copy, 0, 0, 2)
+            e1_slices(V.tensor_copy, 0, 2, 3)
+            e1_quant(0)
+            for h in range(2):
+                e2_copy(0, h, e2_turn(0, h))
+            a_turn(0, 0)
+            a_turn(0, 1)
+            y_turn(0)
+            a_mul(0, 0)
+            a_mul(0, 1)
+            e1_slices(S.copy, 1, 3, 4)
+            e1_slices(V.tensor_copy, 1, 0, 2)
+            e1_slices(V.tensor_copy, 1, 2, 3)
+            a_quant(0, 0)
+            e1_quant(1)
+            a_quant(0, 1)
+            for g in range(G):
+                a_square(0, g)
+            for g in range(G):
+                a_rsqrt(0, g)
+            y_gain(0)
+            mm1(0)
+            for h in range(2):
+                e2_copy(1, h, e2_turn(1, h))
+
+            for c in range(NC):
+                first, last = c == 0, c == NC - 1
+                q_u(c, 0)
+                q_u(c, 1)
+                q_u(c, 2)
+                q_x(c, 0)
+                q_u(c, 3)
+                if first:
+                    q_x(c, 1)
+                    a_pen(0, 0)
+                    a_pen(0, 1)
+                    a_turn(1, 0)
+                    a_turn(1, 1)
+                q_d(c, 0)
+                q_d(c, 1)
+                if not first:
+                    q_x(c, 1)
+                    p_cast(S.copy, c - 1, 1)
+                    for nb in range(NB):
+                        o_turn(c - 1, 0, nb)
+                    for nb in range(NB):
+                        o_copy(S.copy, c - 1, 0, nb)
+                    for nb in range(NB):
+                        o_turn(c - 1, 1, nb)
+                    p_quant(c - 1, 0)
+                q_d(c, 2)
+                q_d(c, 3)
+                if first:
+                    e2_quant(0)
+                if not last:
+                    a_square(c + 1, 0)
+                    a_square(c + 1, 1)
+                if not first:
+                    for nb in range(NB):
+                        o_copy(S.copy, c - 1, 1, nb)
+                        o_store(c - 1, nb, 0, L)
+                if not last:
+                    a_rsqrt(c + 1, 0)
+                    a_rsqrt(c + 1, 1)
+                    a_mul(c + 1, 0)
+                q_q(c)
+                if not last:
+                    a_mul(c + 1, 1)
+                if not first:
+                    p_quant(c - 1, 1)
+                else:
+                    e2_quant(1)
+                q_quant(c)
+                if c == NC - 2:
+                    store_scales(0, C * (NC - 2))
+                if not last:
+                    a_quant(c + 1, 0)
+                    a_quant(c + 1, 1)
+                else:
+                    a_pen(c, 0)
+                    a_pen(c, 1)
+                mm2(c, 0, 0)
+                mm2(c, 0, 1)
+                r_add(c, 0, 0)
+                r_add(c, 0, 1)
+                if not last:
+                    mm1(c + 1)
+                if not last:
+                    if c + 1 < NC - 1:
+                        a_pen(c + 1, 0)
+                mm2(c, 1, 0)
+                if last:
+                    p_cast(V.tensor_copy, c, 0)
+                    for nb in range(NB):
+                        o_turn(c, 0, nb)
+                r_add(c, 1, 0)
+                if not last:
+                    if c + 1 < NC - 1:
+                        a_pen(c + 1, 1)
+                mm2(c, 1, 1)
+                if last:
+                    p_quant(c, 0)
+                    for nb in range(NB):
+                        o_copy(S.copy, c, 0, nb)
+                        o_store(c, nb, 0, 512)
+                r_add(c, 1, 1)
+                if not last:
+                    y_turn(c + 1)
+                    y_gain(c + 1)
+                    p_cast(S.copy, c, 0)
+                    if c + 2 < NC:
+                        a_turn(c + 2, 0)
+                        a_turn(c + 2, 1)
+            c = NC - 1
+            o_turn(c, 1, 0)
+            o_turn(c, 1, 1)
+            p_cast(V.tensor_copy, c, 1)
+            o_copy(S.copy, c, 1, 0)
+            o_store(c, 0, 512, L)
+            o_copy(V.tensor_copy, c, 1, 1)
+            p_quant(c, 1)
+            o_store(c, 1, 512, L)
+            store_scales(C * (NC - 2), N)

@@ -17,95 +17,84 @@ ALU = mybir.AluOpType
 
 P = 128
 G = L // 512
-C = 256
-NC = N // C
-NB = C // P
+B = 256
+CHUNKS = ((0, 256), (256, 512), (768, 256))
 
 
 def tile_polynomialpostnonlinearlibraryunmixinggr_x1_kernel(
     tc, y, a, e, psi, rho, b, out_0, out_1, out_2
 ):
     nc = tc.nc
-    V, S, T = nc.vector, nc.scalar, nc.tensor
+    V, S, T, GP = nc.vector, nc.scalar, nc.tensor, nc.gpsimd
     with ExitStack() as ctx:
         keep = ctx.enter_context(tc.tile_pool(name="keep", bufs=1))
+        one = ctx.enter_context(tc.tile_pool(name="one", bufs=1))
         work = ctx.enter_context(tc.tile_pool(name="work", bufs=2))
         psum = ctx.enter_context(tc.psum_pool(name="psum", bufs=2))
 
-        e_raw, a_raw, y_raw = [], [], []
-        for g in range(G):
-            e_raw.append(keep.tile([P, 4, K], BF16, name="e_raw%d" % g))
-        for c in range(NC):
-            a_raw.append(keep.tile([P, NB, L], BF16, name="a_raw%d" % c))
-            y_raw.append(keep.tile([P, NB, K], BF16, name="y_raw%d" % c))
+        e_raw = [keep.tile([P, 4, K], BF16, name="e_raw%d" % g) for g in range(G)]
+        a_raw = [keep.tile([P, 2, L], BF16, name="a_raw%d" % s) for s in range(4)]
+        y_raw = [keep.tile([P, 2, K], BF16, name="y_raw%d" % s) for s in range(4)]
         b_col = keep.tile([P, 8], BF16, name="b_col")
         psi4 = keep.tile([P, G, 4], BF16, name="psi4")
         rho4 = keep.tile([P, 4], BF16, name="rho4")
-
         ident = keep.tile([P, P], F32, name="ident")
         ident_bf = keep.tile([P, P], BF16, name="ident_bf")
-        make_identity(nc, ident_bf[:])
-        make_identity(nc, ident[:])
-
-        def load_e(g):
-            nc.sync.dma_start(
-                out=e_raw[g][:], in_=e[512 * g : 512 * g + 512, :].rearrange("(p j) k -> p j k", j=4)
-            )
-
-        def load_a(c):
-            nc.sync.dma_start(
-                out=a_raw[c][:], in_=a[C * c : C * c + C, :].rearrange("(r p) l -> p r l", p=P)
-            )
-
-        def load_y(c):
-            nc.sync.dma_start(
-                out=y_raw[c][:], in_=y[C * c : C * c + C, :].rearrange("(r p) k -> p r k", p=P)
-            )
-
         warm = keep.tile([P, 1], F32, name="warm")
         rho_f = keep.tile([P, 4], F32, name="rho_f")
         rho_2 = keep.tile([P, 4], F32, name="rho_2")
+        rho_s = keep.tile([P, 4], F32, name="rho_s")
         rho_h = keep.tile([P, 4], F32, name="rho_h")
         b_all = keep.tile([P, N], BF16, name="b_all")
         e1_codes = keep.tile([P, G, 512], U32, align_bytes=64, name="e1_codes")
         e1_scales = keep.tile([P, G, 512], U8, align_bytes=64, name="e1_scales")
         e2_codes = keep.tile([P, G, 512], U32, align_bytes=64, name="e2_codes")
         e2_scales = keep.tile([P, G, 512], U8, align_bytes=64, name="e2_scales")
-        e1_in = [keep.tile([P, 2048], BF16, align_bytes=64, name="e1_in%d" % g) for g in range(G)]
-        e2_in = [keep.tile([P, 2048], BF16, align_bytes=64, name="e2_in%d" % g) for g in range(G)]
+        e1_in = [work.tile([P, 2048], BF16, align_bytes=64, tag="e_in", name="e1_in%d" % g) for g in range(G)]
+        e2_in = [work.tile([P, 2048], BF16, align_bytes=64, tag="e_in", name="e2_in%d" % g) for g in range(G)]
         p_scales = keep.tile([P, G, N], U8, align_bytes=64, name="p_scales")
 
         at, ap_in, ap_codes, ap_scales, sq, pen = {}, {}, {}, {}, {}, {}
         yt, yr, m1, u2, xx, dd, q_in, q_codes, q_scales = {}, {}, {}, {}, {}, {}, {}, {}, {}
-        h2, res, p_in, o_ps, o_sb = {}, {}, {}, {}, {}
+        h2, res, p_in, o_sb = {}, {}, {}, {}
+        done = set()
+
+        def load_e(g):
+            nc.sync.dma_start(
+                out=e_raw[g][:], in_=e[512 * g : 512 * g + 512, :].rearrange("(p j) k -> p j k", j=4)
+            )
+
+        def load_a(s):
+            nc.sync.dma_start(
+                out=a_raw[s][:], in_=a[B * s : B * s + B, :].rearrange("(r p) l -> p r l", p=P)
+            )
+
+        def load_y(s):
+            nc.sync.dma_start(
+                out=y_raw[s][:], in_=y[B * s : B * s + B, :].rearrange("(r p) k -> p r k", p=P)
+            )
 
         def b_spread():
             bp = psum.tile([P, 8, P], BF16, tag="tp", name="bp")
             for i in range(8):
                 T.transpose(bp[:, i, :], b_col[:, i : i + 1].to_broadcast([P, P]), ident_bf[:])
-            S.copy(
-                out=b_all[:].rearrange("x (p i) -> x p i", i=8),
-                in_=bp[:].rearrange("x i p -> x p i"),
-            )
+            S.copy(out=b_all[:].rearrange("x (p i) -> x p i", i=8), in_=bp[:].rearrange("x i p -> x p i"))
 
-        def e1_slices(eng_copy, g, t0, t1):
-            eng_copy(
-                out=e1_in[g][:].rearrange("p (t m j) -> p t m j", t=4, j=4)[:, t0:t1],
-                in_=e_raw[g][:].rearrange("p j (m t) -> p t m j", t=4)[:, t0:t1],
+        def e1_part(copy, g, m0, m1_):
+            copy(
+                out=e1_in[g][:].rearrange("p (t m j) -> p t m j", t=4, j=4)[:, :, m0:m1_],
+                in_=e_raw[g][:].rearrange("p j (m t) -> p t m j", t=4)[:, :, m0:m1_],
             )
 
         def e1_quant(g):
             V.quantize_mx(out=e1_codes[:, g, :].bitcast(X4), scales=e1_scales[:, g, :], in_=e1_in[g][:])
 
-        def e2_turn(g, h):
+        def e2_make(g, h):
             ep = psum.tile([P, 2, 2, P], F32, tag="tp", name="ep")
             for i in range(2):
                 words = e_raw[g][:, 2 * h + i, :].bitcast(F32)
                 for u in range(2):
                     T.transpose(ep[:, i, u, :], words[:, u:256:2], ident[:])
-            return ep
-
-        def e2_copy(g, h, ep):
             S.copy(
                 out=e2_in[g][:].bitcast(F32).rearrange("p (i m u) -> p i m u", i=4, u=2)[:, 2 * h : 2 * h + 2],
                 in_=ep[:].rearrange("p i u m -> p i m u"),
@@ -114,118 +103,132 @@ def tile_polynomialpostnonlinearlibraryunmixinggr_x1_kernel(
         def e2_quant(g):
             V.quantize_mx(out=e2_codes[:, g, :].bitcast(X4), scales=e2_scales[:, g, :], in_=e2_in[g][:])
 
-        def a_turn(c, g):
-            t = psum.tile([P, 2, C], F32, tag="at", name="at")
-            at[c, g] = t
-            for r in range(NB):
-                words = a_raw[c][:, r, :].bitcast(F32)
+        def a_turn(s, g):
+            t = psum.tile([P, 2, B], F32, tag="at", name="at")
+            at[s, g] = t
+            for r in range(2):
+                words = a_raw[s][:, r, :].bitcast(F32)
                 for u in range(2):
                     T.transpose(
                         t[:, u, P * r : P * r + P], words[:, 256 * g + u : 256 * g + 256 : 2], ident[:]
                     )
 
-        def a_mul(c, g):
-            t = work.tile([P, C, 4], BF16, align_bytes=64, tag="ap_in%d" % g, name="ap_in")
-            ap_in[c, g] = t
+        def a_mul(s, g):
+            if g == 0:
+                ap_in[s] = work.tile([P, G, B, 4], BF16, align_bytes=64, tag="ap_in", name="ap_in")
             V.tensor_tensor(
-                out=t[:].rearrange("p n (u s) -> p n u s", u=2),
-                in0=at[c, g][:].bitcast(BF16).rearrange("p u (n s) -> p n u s", s=2),
-                in1=psi4[:, g, :].rearrange("p (o u s) -> p o u s", o=1, u=2).to_broadcast([P, C, 2, 2]),
+                out=ap_in[s][:, g].rearrange("p n (u d) -> p n u d", u=2),
+                in0=at[s, g][:].bitcast(BF16).rearrange("p u (n d) -> p n u d", d=2),
+                in1=psi4[:, g, :].rearrange("p (o u d) -> p o u d", o=1, u=2).to_broadcast([P, B, 2, 2]),
                 op=ALU.mult,
             )
 
-        def a_quant(c, g):
-            if g == 0:
-                ap_codes[c] = work.tile([P, G, C], U32, align_bytes=64, tag="ap_codes", name="ap_codes")
-                ap_scales[c] = work.tile([P, G, C], U8, align_bytes=64, tag="ap_scales", name="ap_scales")
+        def a_quant(s):
+            ap_codes[s] = work.tile([P, G, B], U32, align_bytes=64, tag="ap_codes", name="ap_codes")
+            ap_scales[s] = work.tile([P, G, B], U8, align_bytes=64, tag="ap_scales", name="ap_scales")
             V.quantize_mx(
-                out=ap_codes[c][:, g, :].bitcast(X4),
-                scales=ap_scales[c][:, g, :],
-                in_=ap_in[c, g][:].rearrange("p n t -> p (n t)"),
+                out=ap_codes[s][:].rearrange("p g n -> p (g n)").bitcast(X4),
+                scales=ap_scales[s][:].rearrange("p g n -> p (g n)"),
+                in_=ap_in[s][:].rearrange("p g n t -> p (g n t)"),
             )
 
-        def flat(c, g):
-            return at[c, g][:].rearrange("p u n -> p (u n)").bitcast(BF16)
+        def flat(s, g):
+            return at[s, g][:].rearrange("p u n -> p (u n)").bitcast(BF16)
 
-        def a_square(c, g):
-            t = work.tile([P, 4 * C], F32, tag="sq%d" % g, name="sq")
-            sq[c, g] = t
-            S.activation(out=t[:], in_=flat(c, g), func=ACT.Square)
+        def a_square(s, g):
+            if g == 0:
+                sq[s] = work.tile([P, G, 4 * B], F32, tag="sq", name="sq")
+            S.activation(out=sq[s][:, g, :], in_=flat(s, g), func=ACT.Square)
 
-        def a_rsqrt(c, g):
-            t = sq[c, g]
-            S.activation(
-                out=t[:], in_=t[:], func=ACT.Abs_reciprocal_sqrt, scale=1.0 / 0.09, bias=0.01 / 0.09
-            )
+        def a_rsqrt(s, g):
+            t = sq[s][:, g, :]
+            S.activation(out=t, in_=t, func=ACT.Abs_reciprocal_sqrt, scale=1.0 / 0.09, bias=0.01 / 0.09)
 
-        def a_pen(c, g):
-            t = work.tile([P, 2, C, 2], F32, tag="pen%d" % g, name="pen")
-            pen[c, g] = t
+        def a_pen(c, s, g):
+            n0, n = CHUNKS[c]
+            r = s - n0 // B
+            if r == 0:
+                pen[c, g] = work.tile([P, 2, n, 2], F32, tag="pen%d" % g, name="pen")
+            done.add((s, g))
             V.tensor_tensor(
-                out=t[:].rearrange("p u n s -> p (u n s)"), in0=flat(c, g), in1=sq[c, g][:], op=ALU.mult
+                out=pen[c, g][:, :, B * r : B * r + B, :].rearrange("p u n d -> p u (n d)"),
+                in0=flat(s, g).rearrange("p (u m) -> p u m", u=2),
+                in1=sq[s][:, g, :].rearrange("p (u m) -> p u m", u=2),
+                op=ALU.mult,
             )
 
-        def y_turn(c):
-            t = psum.tile([P, 2, C], F32, tag="tp", name="yt")
-            yt[c] = t
-            for r in range(NB):
-                words = y_raw[c][:, r, :].bitcast(F32)
-                for u in range(2):
-                    T.transpose(t[:, u, P * r : P * r + P], words[:, u:256:2], ident[:])
-
-        def y_gain(c):
-            t = work.tile([P, 4, C], F32, tag="yr", name="yr")
+        def y_make(c):
+            n0, n = CHUNKS[c]
+            t = one.tile([P, 4, n], F32, tag="yr", name="yr")
             yr[c] = t
-            src = yt[c][:].bitcast(BF16).rearrange("p u (n s) -> p u s n", s=2)
-            for k in range(4):
-                S.activation(
-                    out=t[:, k, :], in_=src[:, k // 2, k % 2, :], func=ACT.Copy, scale=rho_f[:, k : k + 1]
-                )
+            per = 512 // n
+            for h in range(2 // per):
+                ps = psum.tile([P, per, n], F32, tag="tp", name="yt")
+                for i in range(per):
+                    u = per * h + i
+                    for r in range(n // P):
+                        row = n0 // P + r
+                        words = y_raw[row // 2][:, row % 2, :].bitcast(F32)
+                        T.transpose(ps[:, i, P * r : P * r + P], words[:, u:256:2], ident[:])
+                src = ps[:].bitcast(BF16).rearrange("p u (n d) -> p u d n", d=2)
+                for i in range(per):
+                    for d in range(2):
+                        k = 2 * (per * h + i) + d
+                        S.activation(
+                            out=t[:, k, :], in_=src[:, i, d, :], func=ACT.Copy, scale=rho_f[:, k : k + 1]
+                        )
 
         def mm1(c):
-            for h in range(2):
-                t = psum.tile([P, 2, C], F32, tag="m1", name="m1")
-                m1[c, h] = t
-                for i in range(2):
-                    k = 2 * h + i
+            n0, n = CHUNKS[c]
+            per = 512 // n
+            for k in range(4):
+                if k % per == 0:
+                    t = psum.tile([P, per, n], F32, tag="mm", bufs=4, name="m1")
+                m1[c, k] = t
+                for r in range(n // B):
+                    s = n0 // B + r
                     for g in range(G):
                         T.matmul_mx(
-                            out=t[:, i, :],
+                            out=t[:, k % per, B * r : B * r + B],
                             lhsT=e1_codes[:, g, P * k : P * k + P].bitcast(X4),
                             lhsT_scale=e1_scales[:, g, P * k : P * k + P],
-                            rhs=ap_codes[c][:, g, :].bitcast(X4),
-                            rhs_scale=ap_scales[c][:, g, :],
+                            rhs=ap_codes[s][:, g, :].bitcast(X4),
+                            rhs_scale=ap_scales[s][:, g, :],
                             start=(g == 0),
                             stop=(g == G - 1),
                         )
 
         def q_u(c, k):
+            n0, n = CHUNKS[c]
             if k == 0:
-                u2[c] = work.tile([P, 4, C], F32, tag="u2", name="u2")
+                u2[c] = one.tile([P, 4, n], F32, tag="u2", name="u2")
             V.scalar_tensor_tensor(
                 out=u2[c][:, k, :],
-                in0=m1[c, k // 2][:, k % 2, :],
+                in0=m1[c, k][:, k % (512 // n), :],
                 scalar=rho_2[:, k : k + 1],
-                in1=b_all[:, C * c : C * c + C],
+                in1=b_all[:, n0 : n0 + n],
                 op0=ALU.mult,
                 op1=ALU.mult,
             )
 
-        def q_x(c, h):
-            if h == 0:
-                xx[c] = work.tile([P, 4, C], F32, tag="xx", name="xx")
+        def q_x(c, k):
+            n0, n = CHUNKS[c]
+            per = 512 // n
+            if k == 0:
+                xx[c] = one.tile([P, 4, n], F32, tag="xx", name="xx")
             V.scalar_tensor_tensor(
-                out=xx[c][:, 2 * h : 2 * h + 2, :],
-                in0=u2[c][:, 2 * h : 2 * h + 2, :],
+                out=xx[c][:, k : k + per, :],
+                in0=u2[c][:, k : k + per, :],
                 scalar=2.0,
-                in1=m1[c, h][:],
+                in1=m1[c, k][:],
                 op0=ALU.add,
                 op1=ALU.mult,
             )
 
         def q_d(c, k):
+            n0, n = CHUNKS[c]
             if k == 0:
-                dd[c] = work.tile([P, 4, C], F32, tag="dd", name="dd")
+                dd[c] = one.tile([P, 4, n], F32, tag="dd", name="dd")
             V.scalar_tensor_tensor(
                 out=dd[c][:, k, :],
                 in0=xx[c][:, k, :],
@@ -235,58 +238,61 @@ def tile_polynomialpostnonlinearlibraryunmixinggr_x1_kernel(
                 op1=ALU.subtract,
             )
 
-        def q_q(c):
-            t = work.tile([P, C, 4], BF16, align_bytes=64, tag="q_in", name="q_in")
-            q_in[c] = t
+        def q_q(c, r):
+            n0, n = CHUNKS[c]
+            if r == 0:
+                q_in[c] = work.tile([P, n, 4], BF16, align_bytes=64, tag="q_in", name="q_in")
             V.scalar_tensor_tensor(
-                out=t[:],
-                in0=u2[c][:].rearrange("p t n -> p n t"),
+                out=q_in[c][:, B * r : B * r + B, :],
+                in0=u2[c][:, :, B * r : B * r + B].rearrange("p t n -> p n t"),
                 scalar=1.0,
-                in1=dd[c][:].rearrange("p t n -> p n t"),
+                in1=dd[c][:, :, B * r : B * r + B].rearrange("p t n -> p n t"),
                 op0=ALU.add,
                 op1=ALU.mult,
             )
 
         def q_quant(c):
-            q_codes[c] = work.tile([P, C], U32, align_bytes=64, tag="q_codes", name="q_codes")
-            q_scales[c] = work.tile([P, C], U8, align_bytes=64, tag="q_scales", name="q_scales")
+            n0, n = CHUNKS[c]
+            q_codes[c] = work.tile([P, n], U32, align_bytes=64, tag="q_codes", name="q_codes")
+            q_scales[c] = work.tile([P, n], U8, align_bytes=64, tag="q_scales", name="q_scales")
             V.quantize_mx(
                 out=q_codes[c][:].bitcast(X4),
                 scales=q_scales[c][:],
                 in_=q_in[c][:].rearrange("p n t -> p (n t)"),
             )
 
-        def mm2(c, g, h):
-            t = psum.tile([P, 2, C], F32, tag="h2", name="h2")
-            h2[c, g, h] = t
-            for i in range(2):
-                k = 2 * h + i
-                T.matmul_mx(
-                    out=t[:, i, :],
-                    lhsT=e2_codes[:, g, P * k : P * k + P].bitcast(X4),
-                    lhsT_scale=e2_scales[:, g, P * k : P * k + P],
-                    rhs=q_codes[c][:].bitcast(X4),
-                    rhs_scale=q_scales[c][:],
-                    start=True,
-                    stop=True,
-                )
+        def mm2(c, g, k):
+            n0, n = CHUNKS[c]
+            per = 512 // n
+            if k % per == 0:
+                h2[c] = psum.tile([P, per, n], F32, tag="mm", bufs=4, name="h2")
+            h2[c, g, k] = h2[c]
+            T.matmul_mx(
+                out=h2[c][:, k % per, :],
+                lhsT=e2_codes[:, g, P * k : P * k + P].bitcast(X4),
+                lhsT_scale=e2_scales[:, g, P * k : P * k + P],
+                rhs=q_codes[c][:].bitcast(X4),
+                rhs_scale=q_scales[c][:],
+                start=True,
+                stop=True,
+            )
 
-        def r_add(c, g, h):
-            if h == 0:
-                res[c, g] = work.tile([P, 4, C], F32, tag="res%d" % g, name="res")
-            for i in range(2):
-                k = 2 * h + i
-                V.scalar_tensor_tensor(
-                    out=res[c, g][:, k, :],
-                    in0=h2[c, g, h][:, i, :],
-                    scalar=psi4[:, g, k : k + 1],
-                    in1=pen[c, g][:, k // 2, :, k % 2],
-                    op0=ALU.mult,
-                    op1=ALU.add,
-                )
+        def r_add(c, g, k):
+            n0, n = CHUNKS[c]
+            if k == 0:
+                res[c, g] = work.tile([P, 4, n], F32, tag="res%d" % g, name="res")
+            V.scalar_tensor_tensor(
+                out=res[c, g][:, k, :],
+                in0=h2[c, g, k][:, k % (512 // n), :],
+                scalar=psi4[:, g, k : k + 1],
+                in1=pen[c, g][:, k // 2, :, k % 2],
+                op0=ALU.mult,
+                op1=ALU.add,
+            )
 
         def p_cast(copy, c, g):
-            t = work.tile([P, C, 4], BF16, align_bytes=64, tag="p_in%d" % g, name="p_in")
+            n0, n = CHUNKS[c]
+            t = work.tile([P, n, 4], BF16, align_bytes=64, tag="p_in%d" % g, name="p_in")
             p_in[c, g] = t
             copy(
                 out=t[:].rearrange("p (n i) t -> p n t i", i=4),
@@ -294,14 +300,15 @@ def tile_polynomialpostnonlinearlibraryunmixinggr_x1_kernel(
             )
 
         def p_quant(c, g):
-            codes = work.tile([P, C], U32, align_bytes=64, tag="p_codes%d" % g, name="p_codes")
+            n0, n = CHUNKS[c]
+            codes = work.tile([P, n], U32, align_bytes=64, tag="p_codes%d" % g, name="p_codes")
             V.quantize_mx(
                 out=codes[:].bitcast(X4),
-                scales=p_scales[:, g, C * c : C * c + C],
+                scales=p_scales[:, g, n0 : n0 + n],
                 in_=p_in[c, g][:].rearrange("p n t -> p (n t)"),
             )
             nc.sync.dma_start(
-                out=out_1[g, :, C * c : C * c + C, :].rearrange("p m t -> p (m t)").bitcast(I32),
+                out=out_1[g, :, n0 : n0 + n, :].rearrange("p m t -> p (m t)").bitcast(I32),
                 in_=codes[:].bitcast(I32),
             )
 
@@ -312,166 +319,111 @@ def tile_polynomialpostnonlinearlibraryunmixinggr_x1_kernel(
                     in_=p_scales[32 * s : 32 * s + 4, :, n0:n1].bitcast(I32),
                 )
 
-        def o_turn(c, g, nb):
+        def o_make(copy, c, g, nb):
             t = psum.tile([P, 4, P], F32, tag="tp", name="ot")
-            o_ps[c, g, nb] = t
             for k in range(4):
                 T.transpose(t[:, k, :], res[c, g][:, k, P * nb : P * nb + P], ident[:])
-
-        def o_copy(copy, c, g, nb):
             if g == 0:
-                o_sb[c, nb] = work.tile([P, L], F32, tag="o_sb%d" % nb, name="o_sb")
+                o_sb[c, nb] = work.tile([P, L], F32, tag="o_sb", bufs=4, name="o_sb")
             copy(
                 out=o_sb[c, nb][:, 512 * g : 512 * g + 512].rearrange("n (p t) -> n p t", t=4),
-                in_=o_ps[c, g, nb][:].rearrange("n t p -> n p t"),
+                in_=t[:].rearrange("n t p -> n p t"),
             )
 
         def o_store(c, nb, l0, l1):
-            n0 = C * c + P * nb
-            nc.sync.dma_start(out=out_0[n0 : n0 + P, l0:l1], in_=o_sb[c, nb][:, l0:l1])
+            r0 = CHUNKS[c][0] + P * nb
+            nc.sync.dma_start(out=out_0[r0 : r0 + P, l0:l1], in_=o_sb[c, nb][:, l0:l1])
 
-        with tc.manual_schedule():
-            S.dma_start(out=b_col[:], in_=b.rearrange("(p i) -> p i", i=8))
-            S.dma_start(out=rho4[:], in_=rho.rearrange("(p t) -> p t", t=4))
-            S.dma_start(out=psi4[:], in_=psi.rearrange("(g p t) -> p g t", g=G, t=4))
-            load_e(0)
-            load_a(0)
-            load_e(1)
-            load_y(0)
-            for c in range(1, NC):
-                load_a(c)
-                load_y(c)
+        S.dma_start(out=b_col[:], in_=b.rearrange("(p i) -> p i", i=8))
+        S.dma_start(out=psi4[:], in_=psi.rearrange("(g p t) -> p g t", g=G, t=4))
+        S.dma_start(out=rho4[:], in_=rho.rearrange("(p t) -> p t", t=4))
+        load_e(0)
+        load_a(0)
+        load_e(1)
+        load_y(0)
+        for s in range(1, 4):
+            load_a(s)
+            load_y(s)
+        make_identity(nc, ident_bf[:])
+        make_identity(nc, ident[:])
+        GP.memset(warm[:], 1.0)
+        S.activation(out=warm[:], in_=warm[:], func=ACT.Abs_reciprocal_sqrt)
+        GP.tensor_copy(out=rho_f[:], in_=rho4[:])
+        GP.tensor_scalar(out=rho_2[:], in0=rho4[:], scalar1=2.0, scalar2=0.0, op0=ALU.mult, op1=ALU.add)
+        GP.tensor_tensor(out=rho_s[:], in0=rho4[:], in1=rho4[:], op=ALU.mult)
+        GP.tensor_scalar(out=rho_h[:], in0=rho_s[:], scalar1=0.5, scalar2=0.0, op0=ALU.mult, op1=ALU.add)
 
-            V.memset(warm[:], 1.0)
-            S.activation(out=warm[:], in_=warm[:], func=ACT.Abs_reciprocal_sqrt)
-            V.tensor_copy(out=rho_f[:], in_=rho4[:])
-            V.tensor_scalar(out=rho_2[:], in0=rho4[:], scalar1=2.0, scalar2=None, op0=ALU.mult)
-            V.scalar_tensor_tensor(
-                out=rho_h[:], in0=rho4[:], scalar=0.5, in1=rho4[:], op0=ALU.mult, op1=ALU.mult
-            )
-
-            b_spread()
-            e1_slices(S.copy, 0, 3, 4)
-            e1_slices(V.tensor_copy, 0, 0, 2)
-            e1_slices(V.tensor_copy, 0, 2, 3)
-            e1_quant(0)
+        b_spread()
+        e1_part(V.tensor_copy, 0, 0, 96)
+        e1_part(S.copy, 0, 96, 128)
+        e1_quant(0)
+        for g in range(G):
+            a_turn(0, g)
+            a_mul(0, g)
+        a_quant(0)
+        e1_part(V.tensor_copy, 1, 0, 96)
+        e1_part(S.copy, 1, 96, 128)
+        e1_quant(1)
+        mm1(0)
+        for g in range(G):
+            a_square(0, g)
+            a_rsqrt(0, g)
+        y_make(0)
+        for g in range(G):
             for h in range(2):
-                e2_copy(0, h, e2_turn(0, h))
-            a_turn(0, 0)
-            a_turn(0, 1)
-            y_turn(0)
-            a_mul(0, 0)
-            a_mul(0, 1)
-            e1_slices(S.copy, 1, 3, 4)
-            e1_slices(V.tensor_copy, 1, 0, 2)
-            e1_slices(V.tensor_copy, 1, 2, 3)
-            a_quant(0, 0)
-            e1_quant(1)
-            a_quant(0, 1)
-            for g in range(G):
-                a_square(0, g)
-            for g in range(G):
-                a_rsqrt(0, g)
-            y_gain(0)
-            mm1(0)
-            for h in range(2):
-                e2_copy(1, h, e2_turn(1, h))
+                e2_make(g, h)
 
-            for c in range(NC):
-                first, last = c == 0, c == NC - 1
-                q_u(c, 0)
-                q_u(c, 1)
-                q_u(c, 2)
-                q_x(c, 0)
-                q_u(c, 3)
-                if first:
-                    q_x(c, 1)
-                    a_pen(0, 0)
-                    a_pen(0, 1)
-                    a_turn(1, 0)
-                    a_turn(1, 1)
-                q_d(c, 0)
-                q_d(c, 1)
-                if not first:
-                    q_x(c, 1)
-                    p_cast(S.copy, c - 1, 1)
-                    for nb in range(NB):
-                        o_turn(c - 1, 0, nb)
-                    for nb in range(NB):
-                        o_copy(S.copy, c - 1, 0, nb)
-                    for nb in range(NB):
-                        o_turn(c - 1, 1, nb)
-                    p_quant(c - 1, 0)
-                q_d(c, 2)
-                q_d(c, 3)
-                if first:
-                    e2_quant(0)
-                if not last:
-                    a_square(c + 1, 0)
-                    a_square(c + 1, 1)
-                if not first:
-                    for nb in range(NB):
-                        o_copy(S.copy, c - 1, 1, nb)
-                        o_store(c - 1, nb, 0, L)
-                if not last:
-                    a_rsqrt(c + 1, 0)
-                    a_rsqrt(c + 1, 1)
-                    a_mul(c + 1, 0)
-                q_q(c)
-                if not last:
-                    a_mul(c + 1, 1)
-                if not first:
-                    p_quant(c - 1, 1)
-                else:
-                    e2_quant(1)
-                q_quant(c)
-                if c == NC - 2:
-                    store_scales(0, C * (NC - 2))
-                if not last:
-                    a_quant(c + 1, 0)
-                    a_quant(c + 1, 1)
-                else:
-                    a_pen(c, 0)
-                    a_pen(c, 1)
-                mm2(c, 0, 0)
-                mm2(c, 0, 1)
-                r_add(c, 0, 0)
-                r_add(c, 0, 1)
-                if not last:
-                    mm1(c + 1)
-                if not last:
-                    if c + 1 < NC - 1:
-                        a_pen(c + 1, 0)
-                mm2(c, 1, 0)
-                if last:
-                    p_cast(V.tensor_copy, c, 0)
-                    for nb in range(NB):
-                        o_turn(c, 0, nb)
-                r_add(c, 1, 0)
-                if not last:
-                    if c + 1 < NC - 1:
-                        a_pen(c + 1, 1)
-                mm2(c, 1, 1)
-                if last:
-                    p_quant(c, 0)
-                    for nb in range(NB):
-                        o_copy(S.copy, c, 0, nb)
-                        o_store(c, nb, 0, 512)
-                r_add(c, 1, 1)
-                if not last:
-                    y_turn(c + 1)
-                    y_gain(c + 1)
-                    p_cast(S.copy, c, 0)
-                    if c + 2 < NC:
-                        a_turn(c + 2, 0)
-                        a_turn(c + 2, 1)
-            c = NC - 1
-            o_turn(c, 1, 0)
-            o_turn(c, 1, 1)
-            p_cast(V.tensor_copy, c, 1)
-            o_copy(S.copy, c, 1, 0)
-            o_store(c, 0, 512, L)
-            o_copy(V.tensor_copy, c, 1, 1)
-            p_quant(c, 1)
-            o_store(c, 1, 512, L)
-            store_scales(C * (NC - 2), N)
+        NCH = len(CHUNKS)
+        for c in range(NCH):
+            n0, n = CHUNKS[c]
+            last = c == NCH - 1
+            per = 512 // n
+            for k in range(4):
+                q_u(c, k)
+                if k % per == per - 1 and k >= 1:
+                    q_x(c, k - per + 1 if per > 1 else k - 1)
+            if per == 1:
+                q_x(c, 3)
+            for k in range(4):
+                q_d(c, k)
+            for r in range(n // B):
+                q_q(c, r)
+            q_quant(c)
+            subs = [n0 // B + r for r in range(n // B)]
+            for s in subs:
+                for g in range(G):
+                    if (s, g) not in done:
+                        a_pen(c, s, g)
+            if c == 0:
+                e2_quant(0)
+                e2_quant(1)
+            nxt = [] if last else [CHUNKS[c + 1][0] // B + r for r in range(CHUNKS[c + 1][1] // B)]
+            for s in nxt:
+                for g in range(G):
+                    a_turn(s, g)
+                    a_mul(s, g)
+                    a_square(s, g)
+                    a_rsqrt(s, g)
+                a_quant(s)
+                if s != nxt[-1]:
+                    for g in range(G):
+                        a_pen(c + 1, s, g)
+            for g in range(G):
+                for k in range(4):
+                    mm2(c, g, k)
+                    r_add(c, g, k)
+            if not last:
+                y_make(c + 1)
+                mm1(c + 1)
+            for g in range(G):
+                p_cast(V.tensor_copy if last else S.copy, c, g)
+                for nb in range(n // P):
+                    o_make(V.tensor_copy if last and g == 1 and nb == 1 else S.copy, c, g, nb)
+                    if last:
+                        o_store(c, nb, 512 * g, 512 * g + 512)
+                    elif g == 1:
+                        o_store(c, nb, 0, L)
+                p_quant(c, g)
+            if c == NCH - 2:
+                store_scales(0, CHUNKS[-1][0])
+        store_scales(CHUNKS[-1][0], N)

@@ -55,9 +55,8 @@ def tile_polynomialpostnonlinearlibraryunmixinggr_x1_kernel(
         p_scales = keep.tile([P, G, N], U8, align_bytes=64, name="p_scales")
 
         at, ap_in, ap_codes, ap_scales, sq, pen = {}, {}, {}, {}, {}, {}
-        yt, yr, m1, u2, xx, dd, q_in, q_codes, q_scales = {}, {}, {}, {}, {}, {}, {}, {}, {}
-        h2, res, p_in, o_sb = {}, {}, {}, {}
-        done = set()
+        yt, yr, m1, u2, xx, q_in, q_codes, q_scales = {}, {}, {}, {}, {}, {}, {}, {}
+        h2, res, p_in, o_sb, o_ps, e2_ps = {}, {}, {}, {}, {}, {}
 
         def load_e(g):
             nc.sync.dma_start(
@@ -89,12 +88,16 @@ def tile_polynomialpostnonlinearlibraryunmixinggr_x1_kernel(
         def e1_quant(g):
             V.quantize_mx(out=e1_codes[:, g, :].bitcast(X4), scales=e1_scales[:, g, :], in_=e1_in[g][:])
 
-        def e2_make(g, h):
+        def e2_turn(g, h):
             ep = psum.tile([P, 2, 2, P], F32, tag="tp", name="ep")
             for i in range(2):
                 words = e_raw[g][:, 2 * h + i, :].bitcast(F32)
                 for u in range(2):
                     T.transpose(ep[:, i, u, :], words[:, u:256:2], ident[:])
+            e2_ps[g, h] = ep
+
+        def e2_copy(g, h):
+            ep = e2_ps[g, h]
             S.copy(
                 out=e2_in[g][:].bitcast(F32).rearrange("p (i m u) -> p i m u", i=4, u=2)[:, 2 * h : 2 * h + 2],
                 in_=ep[:].rearrange("p i u m -> p i m u"),
@@ -132,51 +135,48 @@ def tile_polynomialpostnonlinearlibraryunmixinggr_x1_kernel(
                 in_=ap_in[s][:].rearrange("p g n t -> p (g n t)"),
             )
 
-        def flat(s, g):
-            return at[s, g][:].rearrange("p u n -> p (u n)").bitcast(BF16)
+        def by_t(s, g):
+            return at[s, g][:].bitcast(BF16).rearrange("p u (n d) -> p u d n", d=2)
 
         def a_square(s, g):
             if g == 0:
-                sq[s] = work.tile([P, G, 4 * B], F32, tag="sq", name="sq")
-            S.activation(out=sq[s][:, g, :], in_=flat(s, g), func=ACT.Square)
+                sq[s] = work.tile([P, G, 2, 2, B], F32, tag="sq", name="sq")
+            S.activation(out=sq[s][:, g], in_=by_t(s, g), func=ACT.Square)
 
         def a_rsqrt(s, g):
-            t = sq[s][:, g, :]
+            t = sq[s][:, g].rearrange("p u d n -> p (u d n)")
             S.activation(out=t, in_=t, func=ACT.Abs_reciprocal_sqrt, scale=1.0 / 0.09, bias=0.01 / 0.09)
 
         def a_pen(c, s, g):
             n0, n = CHUNKS[c]
             r = s - n0 // B
             if r == 0:
-                pen[c, g] = work.tile([P, 2, n, 2], F32, tag="pen%d" % g, name="pen")
-            done.add((s, g))
+                pen[c, g] = work.tile([P, 2, 2, n], F32, tag="pen%d" % g, name="pen")
             V.tensor_tensor(
-                out=pen[c, g][:, :, B * r : B * r + B, :].rearrange("p u n d -> p u (n d)"),
-                in0=flat(s, g).rearrange("p (u m) -> p u m", u=2),
-                in1=sq[s][:, g, :].rearrange("p (u m) -> p u m", u=2),
-                op=ALU.mult,
+                out=pen[c, g][:, :, :, B * r : B * r + B], in0=by_t(s, g), in1=sq[s][:, g], op=ALU.mult
             )
 
-        def y_make(c):
+        def y_turn(c):
             n0, n = CHUNKS[c]
-            t = one.tile([P, 4, n], F32, tag="yr", name="yr")
-            yr[c] = t
             per = 512 // n
-            for h in range(2 // per):
-                ps = psum.tile([P, per, n], F32, tag="tp", name="yt")
-                for i in range(per):
-                    u = per * h + i
-                    for r in range(n // P):
-                        row = n0 // P + r
-                        words = y_raw[row // 2][:, row % 2, :].bitcast(F32)
-                        T.transpose(ps[:, i, P * r : P * r + P], words[:, u:256:2], ident[:])
-                src = ps[:].bitcast(BF16).rearrange("p u (n d) -> p u d n", d=2)
-                for i in range(per):
-                    for d in range(2):
-                        k = 2 * (per * h + i) + d
-                        S.activation(
-                            out=t[:, k, :], in_=src[:, i, d, :], func=ACT.Copy, scale=rho_f[:, k : k + 1]
-                        )
+            for u in range(2):
+                if u % per == 0:
+                    ps = psum.tile([P, per, n], F32, tag="tp", name="yt")
+                yt[c, u] = ps
+                for r in range(n // P):
+                    row = n0 // P + r
+                    words = y_raw[row // 2][:, row % 2, :].bitcast(F32)
+                    T.transpose(ps[:, u % per, P * r : P * r + P], words[:, u:256:2], ident[:])
+
+        def y_gain(c, k):
+            n0, n = CHUNKS[c]
+            if k == 0:
+                yr[c] = one.tile([P, 4, n], F32, tag="yr", name="yr")
+            u, d = k // 2, k % 2
+            src = yt[c, u][:].bitcast(BF16).rearrange("p u (n d) -> p u d n", d=2)
+            S.activation(
+                out=yr[c][:, k, :], in_=src[:, u % (512 // n), d, :], func=ACT.Copy, scale=rho_f[:, k : k + 1]
+            )
 
         def mm1(c):
             n0, n = CHUNKS[c]
@@ -227,10 +227,8 @@ def tile_polynomialpostnonlinearlibraryunmixinggr_x1_kernel(
 
         def q_d(c, k):
             n0, n = CHUNKS[c]
-            if k == 0:
-                dd[c] = one.tile([P, 4, n], F32, tag="dd", name="dd")
             V.scalar_tensor_tensor(
-                out=dd[c][:, k, :],
+                out=xx[c][:, k, :],
                 in0=xx[c][:, k, :],
                 scalar=rho_h[:, k : k + 1],
                 in1=yr[c][:, k, :],
@@ -246,7 +244,7 @@ def tile_polynomialpostnonlinearlibraryunmixinggr_x1_kernel(
                 out=q_in[c][:, B * r : B * r + B, :],
                 in0=u2[c][:, :, B * r : B * r + B].rearrange("p t n -> p n t"),
                 scalar=1.0,
-                in1=dd[c][:, :, B * r : B * r + B].rearrange("p t n -> p n t"),
+                in1=xx[c][:, :, B * r : B * r + B].rearrange("p t n -> p n t"),
                 op0=ALU.add,
                 op1=ALU.mult,
             )
@@ -285,7 +283,7 @@ def tile_polynomialpostnonlinearlibraryunmixinggr_x1_kernel(
                 out=res[c, g][:, k, :],
                 in0=h2[c, g, k][:, k % (512 // n), :],
                 scalar=psi4[:, g, k : k + 1],
-                in1=pen[c, g][:, k // 2, :, k % 2],
+                in1=pen[c, g][:, k // 2, k % 2, :],
                 op0=ALU.mult,
                 op1=ALU.add,
             )
@@ -319,111 +317,216 @@ def tile_polynomialpostnonlinearlibraryunmixinggr_x1_kernel(
                     in_=p_scales[32 * s : 32 * s + 4, :, n0:n1].bitcast(I32),
                 )
 
-        def o_make(copy, c, g, nb):
+        def o_turn(c, g, nb):
             t = psum.tile([P, 4, P], F32, tag="tp", name="ot")
+            o_ps[c, g, nb] = t
             for k in range(4):
                 T.transpose(t[:, k, :], res[c, g][:, k, P * nb : P * nb + P], ident[:])
+
+        def o_copy(copy, c, g, nb):
             if g == 0:
-                o_sb[c, nb] = work.tile([P, L], F32, tag="o_sb", bufs=4, name="o_sb")
+                o_sb[c, nb] = work.tile([P, L], F32, tag="o_sb", bufs=6, name="o_sb")
             copy(
                 out=o_sb[c, nb][:, 512 * g : 512 * g + 512].rearrange("n (p t) -> n p t", t=4),
-                in_=t[:].rearrange("n t p -> n p t"),
+                in_=o_ps[c, g, nb][:].rearrange("n t p -> n p t"),
             )
 
         def o_store(c, nb, l0, l1):
             r0 = CHUNKS[c][0] + P * nb
             nc.sync.dma_start(out=out_0[r0 : r0 + P, l0:l1], in_=o_sb[c, nb][:, l0:l1])
 
-        S.dma_start(out=b_col[:], in_=b.rearrange("(p i) -> p i", i=8))
-        S.dma_start(out=psi4[:], in_=psi.rearrange("(g p t) -> p g t", g=G, t=4))
-        S.dma_start(out=rho4[:], in_=rho.rearrange("(p t) -> p t", t=4))
-        load_e(0)
-        load_a(0)
-        load_e(1)
-        load_y(0)
-        for s in range(1, 4):
-            load_a(s)
-            load_y(s)
         make_identity(nc, ident_bf[:])
         make_identity(nc, ident[:])
-        GP.memset(warm[:], 1.0)
-        S.activation(out=warm[:], in_=warm[:], func=ACT.Abs_reciprocal_sqrt)
-        GP.tensor_copy(out=rho_f[:], in_=rho4[:])
-        GP.tensor_scalar(out=rho_2[:], in0=rho4[:], scalar1=2.0, scalar2=0.0, op0=ALU.mult, op1=ALU.add)
-        GP.tensor_tensor(out=rho_s[:], in0=rho4[:], in1=rho4[:], op=ALU.mult)
-        GP.tensor_scalar(out=rho_h[:], in0=rho_s[:], scalar1=0.5, scalar2=0.0, op0=ALU.mult, op1=ALU.add)
+        VC, SC = V.tensor_copy, S.copy
+        with tc.manual_schedule():
+            S.dma_start(out=b_col[:], in_=b.rearrange("(p i) -> p i", i=8))
+            S.dma_start(out=psi4[:], in_=psi.rearrange("(g p t) -> p g t", g=G, t=4))
+            S.dma_start(out=rho4[:], in_=rho.rearrange("(p t) -> p t", t=4))
+            load_e(0)
+            load_a(0)
+            load_e(1)
+            load_y(0)
+            for s in range(1, 4):
+                load_a(s)
+                load_y(s)
+            GP.memset(warm[:], 1.0)
+            S.activation(out=warm[:], in_=warm[:], func=ACT.Abs_reciprocal_sqrt)
+            GP.tensor_copy(out=rho_f[:], in_=rho4[:])
+            GP.tensor_scalar(out=rho_2[:], in0=rho4[:], scalar1=2.0, scalar2=0.0, op0=ALU.mult, op1=ALU.add)
+            GP.tensor_tensor(out=rho_s[:], in0=rho4[:], in1=rho4[:], op=ALU.mult)
+            GP.tensor_scalar(out=rho_h[:], in0=rho_s[:], scalar1=0.5, scalar2=0.0, op0=ALU.mult, op1=ALU.add)
 
-        b_spread()
-        e1_part(V.tensor_copy, 0, 0, 96)
-        e1_part(S.copy, 0, 96, 128)
-        e1_quant(0)
-        for g in range(G):
-            a_turn(0, g)
-            a_mul(0, g)
-        a_quant(0)
-        e1_part(V.tensor_copy, 1, 0, 96)
-        e1_part(S.copy, 1, 96, 128)
-        e1_quant(1)
-        mm1(0)
-        for g in range(G):
-            a_square(0, g)
-            a_rsqrt(0, g)
-        y_make(0)
-        for g in range(G):
-            for h in range(2):
-                e2_make(g, h)
+            b_spread()
+            e1_part(VC, 0, 0, 96)
+            e1_part(SC, 0, 96, 128)
+            e2_turn(0, 0)
+            e2_copy(0, 0)
+            e2_turn(0, 1)
+            e2_copy(0, 1)
+            e1_quant(0)
+            a_turn(0, 0)
+            a_turn(0, 1)
+            a_mul(0, 0)
+            a_mul(0, 1)
+            e1_part(VC, 1, 0, 96)
+            e1_part(SC, 1, 96, 128)
+            a_quant(0)
+            e1_quant(1)
+            a_square(0, 0)
+            a_square(0, 1)
+            y_turn(0)
+            mm1(0)
+            a_rsqrt(0, 0)
+            a_rsqrt(0, 1)
+            for k in range(4):
+                y_gain(0, k)
+            e2_turn(1, 0)
+            e2_copy(1, 0)
+            e2_turn(1, 1)
+            e2_copy(1, 1)
 
-        NCH = len(CHUNKS)
-        for c in range(NCH):
-            n0, n = CHUNKS[c]
-            last = c == NCH - 1
-            per = 512 // n
+            q_u(0, 0)
+            q_u(0, 1)
+            q_u(0, 2)
+            q_x(0, 0)
+            q_u(0, 3)
+            a_pen(0, 0, 0)
+            q_x(0, 2)
+            a_pen(0, 0, 1)
+            a_turn(1, 0)
+            a_turn(1, 1)
             for k in range(4):
-                q_u(c, k)
-                if k % per == per - 1 and k >= 1:
-                    q_x(c, k - per + 1 if per > 1 else k - 1)
-            if per == 1:
-                q_x(c, 3)
-            for k in range(4):
-                q_d(c, k)
-            for r in range(n // B):
-                q_q(c, r)
-            q_quant(c)
-            subs = [n0 // B + r for r in range(n // B)]
-            for s in subs:
-                for g in range(G):
-                    if (s, g) not in done:
-                        a_pen(c, s, g)
-            if c == 0:
-                e2_quant(0)
-                e2_quant(1)
-            nxt = [] if last else [CHUNKS[c + 1][0] // B + r for r in range(CHUNKS[c + 1][1] // B)]
-            for s in nxt:
-                for g in range(G):
-                    a_turn(s, g)
-                    a_mul(s, g)
-                    a_square(s, g)
-                    a_rsqrt(s, g)
-                a_quant(s)
-                if s != nxt[-1]:
-                    for g in range(G):
-                        a_pen(c + 1, s, g)
+                q_d(0, k)
+            a_square(1, 0)
+            a_square(1, 1)
+            e2_quant(0)
+            a_mul(1, 0)
+            q_q(0, 0)
+            a_mul(1, 1)
+            e2_quant(1)
+            q_quant(0)
+            a_rsqrt(1, 0)
+            a_rsqrt(1, 1)
+            a_quant(1)
+            y_turn(1)
             for g in range(G):
                 for k in range(4):
-                    mm2(c, g, k)
-                    r_add(c, g, k)
-            if not last:
-                y_make(c + 1)
-                mm1(c + 1)
+                    mm2(0, g, k)
+            for k in range(4):
+                y_gain(1, k)
+            a_pen(1, 1, 0)
+            a_turn(2, 0)
+            for k in range(4):
+                r_add(0, 0, k)
+            a_pen(1, 1, 1)
+            a_turn(2, 1)
+            a_mul(2, 0)
+            a_square(2, 0)
+            r_add(0, 1, 0)
+            r_add(0, 1, 1)
+            a_mul(2, 1)
+            a_square(2, 1)
+            p_cast(SC, 0, 0)
+            r_add(0, 1, 2)
+            a_quant(2)
+            r_add(0, 1, 3)
+            mm1(1)
+            p_cast(SC, 0, 1)
+            a_rsqrt(2, 0)
+            a_rsqrt(2, 1)
+            for nb in range(2):
+                o_turn(0, 0, nb)
+                o_copy(SC, 0, 0, nb)
+
+            q_u(1, 0)
+            q_u(1, 1)
+            q_x(1, 0)
+            p_quant(0, 0)
+            q_u(1, 2)
+            q_x(1, 1)
+            p_quant(0, 1)
+            q_u(1, 3)
+            q_x(1, 2)
+            a_pen(1, 2, 0)
+            q_x(1, 3)
+            a_pen(1, 2, 1)
+            for nb in range(2):
+                o_turn(0, 1, nb)
+                o_copy(SC, 0, 1, nb)
+                o_store(0, nb, 0, L)
+            a_turn(3, 0)
+            a_turn(3, 1)
+            for k in range(4):
+                q_d(1, k)
+            a_square(3, 0)
+            a_square(3, 1)
+            a_mul(3, 0)
+            q_q(1, 0)
+            q_q(1, 1)
+            a_mul(3, 1)
+            q_quant(1)
+            a_rsqrt(3, 0)
+            a_rsqrt(3, 1)
+            y_turn(2)
+            for k in range(4):
+                y_gain(2, k)
+            a_quant(3)
+            a_pen(2, 3, 0)
+            for k in range(4):
+                mm2(1, 0, k)
+            for k in range(4):
+                r_add(1, 0, k)
+                mm2(1, 1, k)
+            p_cast(SC, 1, 0)
+            mm1(2)
+            for nb in range(4):
+                o_turn(1, 0, nb)
+                o_copy(SC, 1, 0, nb)
+            for k in range(4):
+                r_add(1, 1, k)
+
+            q_u(2, 0)
+            q_u(2, 1)
+            q_u(2, 2)
+            q_x(2, 0)
+            q_u(2, 3)
+            q_d(2, 0)
+            q_d(2, 1)
+            q_x(2, 2)
+            p_cast(VC, 1, 1)
+            q_d(2, 2)
+            q_d(2, 3)
+            p_quant(1, 0)
+            q_q(2, 0)
+            p_quant(1, 1)
+            q_quant(2)
+            store_scales(0, 768)
+            for nb in range(4):
+                o_turn(1, 1, nb)
+                o_copy(SC, 1, 1, nb)
+                o_store(1, nb, 0, L)
+            a_pen(2, 3, 1)
             for g in range(G):
-                p_cast(V.tensor_copy if last else S.copy, c, g)
-                for nb in range(n // P):
-                    o_make(V.tensor_copy if last and g == 1 and nb == 1 else S.copy, c, g, nb)
-                    if last:
-                        o_store(c, nb, 512 * g, 512 * g + 512)
-                    elif g == 1:
-                        o_store(c, nb, 0, L)
-                p_quant(c, g)
-            if c == NCH - 2:
-                store_scales(0, CHUNKS[-1][0])
-        store_scales(CHUNKS[-1][0], N)
+                for k in range(4):
+                    mm2(2, g, k)
+            for k in range(4):
+                r_add(2, 0, k)
+            r_add(2, 1, 0)
+            p_cast(VC, 2, 0)
+            for nb in range(2):
+                o_turn(2, 0, nb)
+                o_copy(SC, 2, 0, nb)
+                o_store(2, nb, 0, 512)
+            r_add(2, 1, 1)
+            r_add(2, 1, 2)
+            p_quant(2, 0)
+            r_add(2, 1, 3)
+            for nb in range(2):
+                o_turn(2, 1, nb)
+            o_copy(SC, 2, 1, 0)
+            o_store(2, 0, 512, L)
+            o_copy(VC, 2, 1, 1)
+            o_store(2, 1, 512, L)
+            p_cast(VC, 2, 1)
+            p_quant(2, 1)
+            store_scales(768, N)

@@ -54,7 +54,7 @@ def tile_polynomialpostnonlinearlibraryunmixinggr_x1_kernel(
         e2_in = [work.tile([P, 2048], BF16, align_bytes=64, tag="e_in", name="e2_in%d" % g) for g in range(G)]
         p_scales = keep.tile([P, G, N], U8, align_bytes=64, name="p_scales")
 
-        at, ap_in, ap_codes, ap_scales, sq, pen = {}, {}, {}, {}, {}, {}
+        at, a_t, ap_in, ap_codes, ap_scales, pen = {}, {}, {}, {}, {}, {}
         yt, yr, m1, u2, xx, q_in, q_codes, q_scales = {}, {}, {}, {}, {}, {}, {}, {}
         h2, res, p_in, o_sb, o_ps, e2_ps = {}, {}, {}, {}, {}, {}
 
@@ -117,7 +117,7 @@ def tile_polynomialpostnonlinearlibraryunmixinggr_x1_kernel(
                     )
 
         def a_mul(s, g):
-            if g == 0:
+            if s not in ap_in:
                 ap_in[s] = work.tile([P, G, B, 4], BF16, align_bytes=64, tag="ap_in", name="ap_in")
             V.tensor_tensor(
                 out=ap_in[s][:, g].rearrange("p n (u d) -> p n u d", u=2),
@@ -135,26 +135,40 @@ def tile_polynomialpostnonlinearlibraryunmixinggr_x1_kernel(
                 in_=ap_in[s][:].rearrange("p g n t -> p (g n t)"),
             )
 
-        def by_t(s, g):
-            return at[s, g][:].bitcast(BF16).rearrange("p u (n d) -> p u d n", d=2)
+        def raw_t(s, g):
+            return at[s, g][:].bitcast(BF16)
+
+        def pen_part(s, g):
+            c = [i for i, (n0, n) in enumerate(CHUNKS) if n0 <= B * s < n0 + n][0]
+            n0, n = CHUNKS[c]
+            if (c, g) not in pen:
+                pen[c, g] = work.tile([P, 2, n, 2], F32, tag="pen%d" % g, name="pen")
+            r = s - n0 // B
+            return pen[c, g][:, :, B * r : B * r + B, :].rearrange("p u n d -> p u (n d)")
+
+        def a_hold(s, g):
+            if s not in a_t:
+                a_t[s] = work.tile([P, G, 2, B], F32, align_bytes=64, tag="a_t", name="a_t")
+            S.copy(out=a_t[s][:, g], in_=at[s, g][:])
 
         def a_square(s, g):
-            if g == 0:
-                sq[s] = work.tile([P, G, 2, 2, B], F32, tag="sq", name="sq")
-            S.activation(out=sq[s][:, g], in_=by_t(s, g), func=ACT.Square)
+            S.activation(out=pen_part(s, g), in_=raw_t(s, g), func=ACT.Square)
 
         def a_rsqrt(s, g):
-            t = sq[s][:, g].rearrange("p u d n -> p (u d n)")
+            t = pen_part(s, g)
             S.activation(out=t, in_=t, func=ACT.Abs_reciprocal_sqrt, scale=1.0 / 0.09, bias=0.01 / 0.09)
 
-        def a_pen(c, s, g):
-            n0, n = CHUNKS[c]
-            r = s - n0 // B
-            if r == 0:
-                pen[c, g] = work.tile([P, 2, 2, n], F32, tag="pen%d" % g, name="pen")
-            V.tensor_tensor(
-                out=pen[c, g][:, :, :, B * r : B * r + B], in0=by_t(s, g), in1=sq[s][:, g], op=ALU.mult
-            )
+        def a_pen(s, g):
+            t = pen_part(s, g)
+            V.tensor_tensor(out=t, in0=raw_t(s, g), in1=t, op=ALU.mult)
+
+        def a_pen_gp(s, g):
+            t = pen_part(s, g)
+            src = a_t[s][:, g].bitcast(BF16)
+            for u in range(2):
+                for h in range(2):
+                    w = slice(B * h, B * h + B)
+                    GP.tensor_tensor(out=t[:, u, w], in0=src[:, u, w], in1=t[:, u, w], op=ALU.mult)
 
         def y_turn(c):
             n0, n = CHUNKS[c]
@@ -170,7 +184,7 @@ def tile_polynomialpostnonlinearlibraryunmixinggr_x1_kernel(
 
         def y_gain(c, k):
             n0, n = CHUNKS[c]
-            if k == 0:
+            if c not in yr:
                 yr[c] = one.tile([P, 4, n], F32, tag="yr", name="yr")
             u, d = k // 2, k % 2
             src = yt[c, u][:].bitcast(BF16).rearrange("p u (n d) -> p u d n", d=2)
@@ -200,8 +214,8 @@ def tile_polynomialpostnonlinearlibraryunmixinggr_x1_kernel(
 
         def q_u(c, k):
             n0, n = CHUNKS[c]
-            if k == 0:
-                u2[c] = one.tile([P, 4, n], F32, tag="u2", name="u2")
+            if c not in u2:
+                u2[c] = work.tile([P, 4, n], F32, tag="u2", name="u2")
             V.scalar_tensor_tensor(
                 out=u2[c][:, k, :],
                 in0=m1[c, k][:, k % (512 // n), :],
@@ -214,7 +228,7 @@ def tile_polynomialpostnonlinearlibraryunmixinggr_x1_kernel(
         def q_x(c, k):
             n0, n = CHUNKS[c]
             per = 512 // n
-            if k == 0:
+            if c not in xx:
                 xx[c] = one.tile([P, 4, n], F32, tag="xx", name="xx")
             V.scalar_tensor_tensor(
                 out=xx[c][:, k : k + per, :],
@@ -238,7 +252,7 @@ def tile_polynomialpostnonlinearlibraryunmixinggr_x1_kernel(
 
         def q_q(c, r):
             n0, n = CHUNKS[c]
-            if r == 0:
+            if c not in q_in:
                 q_in[c] = work.tile([P, n, 4], BF16, align_bytes=64, tag="q_in", name="q_in")
             V.scalar_tensor_tensor(
                 out=q_in[c][:, B * r : B * r + B, :],
@@ -262,11 +276,10 @@ def tile_polynomialpostnonlinearlibraryunmixinggr_x1_kernel(
         def mm2(c, g, k):
             n0, n = CHUNKS[c]
             per = 512 // n
-            if k % per == 0:
-                h2[c] = psum.tile([P, per, n], F32, tag="mm", bufs=4, name="h2")
-            h2[c, g, k] = h2[c]
+            if (c, g, k // per) not in h2:
+                h2[c, g, k // per] = psum.tile([P, per, n], F32, tag="mm", bufs=4, name="h2")
             T.matmul_mx(
-                out=h2[c][:, k % per, :],
+                out=h2[c, g, k // per][:, k % per, :],
                 lhsT=e2_codes[:, g, P * k : P * k + P].bitcast(X4),
                 lhsT_scale=e2_scales[:, g, P * k : P * k + P],
                 rhs=q_codes[c][:].bitcast(X4),
@@ -277,13 +290,13 @@ def tile_polynomialpostnonlinearlibraryunmixinggr_x1_kernel(
 
         def r_add(c, g, k):
             n0, n = CHUNKS[c]
-            if k == 0:
+            if (c, g) not in res:
                 res[c, g] = work.tile([P, 4, n], F32, tag="res%d" % g, name="res")
             V.scalar_tensor_tensor(
                 out=res[c, g][:, k, :],
-                in0=h2[c, g, k][:, k % (512 // n), :],
+                in0=h2[c, g, k // (512 // n)][:, k % (512 // n), :],
                 scalar=psi4[:, g, k : k + 1],
-                in1=pen[c, g][:, k // 2, k % 2, :],
+                in1=pen[c, g][:, k // 2, :, k % 2],
                 op0=ALU.mult,
                 op1=ALU.add,
             )
@@ -324,7 +337,7 @@ def tile_polynomialpostnonlinearlibraryunmixinggr_x1_kernel(
                 T.transpose(t[:, k, :], res[c, g][:, k, P * nb : P * nb + P], ident[:])
 
         def o_copy(copy, c, g, nb):
-            if g == 0:
+            if (c, nb) not in o_sb:
                 o_sb[c, nb] = work.tile([P, L], F32, tag="o_sb", bufs=6, name="o_sb")
             copy(
                 out=o_sb[c, nb][:, 512 * g : 512 * g + 512].rearrange("n (p t) -> n p t", t=4),
@@ -356,177 +369,233 @@ def tile_polynomialpostnonlinearlibraryunmixinggr_x1_kernel(
             GP.tensor_tensor(out=rho_s[:], in0=rho4[:], in1=rho4[:], op=ALU.mult)
             GP.tensor_scalar(out=rho_h[:], in0=rho_s[:], scalar1=0.5, scalar2=0.0, op0=ALU.mult, op1=ALU.add)
 
-            b_spread()
             e1_part(VC, 0, 0, 96)
-            e1_part(SC, 0, 96, 128)
+            b_spread()
             e2_turn(0, 0)
+            e1_part(SC, 0, 96, 128)
             e2_copy(0, 0)
-            e2_turn(0, 1)
-            e2_copy(0, 1)
             e1_quant(0)
             a_turn(0, 0)
+            e2_turn(0, 1)
             a_turn(0, 1)
+            y_turn(0)
             a_mul(0, 0)
-            a_mul(0, 1)
             e1_part(VC, 1, 0, 96)
             e1_part(SC, 1, 96, 128)
-            a_quant(0)
             e1_quant(1)
+            a_turn(1, 0)
+            a_hold(0, 0)
             a_square(0, 0)
-            a_square(0, 1)
-            y_turn(0)
+            e2_copy(0, 1)
+            a_mul(0, 1)
+            a_quant(0)
             mm1(0)
-            a_rsqrt(0, 0)
-            a_rsqrt(0, 1)
-            for k in range(4):
-                y_gain(0, k)
             e2_turn(1, 0)
-            e2_copy(1, 0)
+            a_turn(1, 1)
+            a_rsqrt(0, 0)
+            e2_quant(0)
+            y_gain(0, 0)
             e2_turn(1, 1)
-            e2_copy(1, 1)
-
             q_u(0, 0)
             q_u(0, 1)
-            q_u(0, 2)
-            q_x(0, 0)
-            q_u(0, 3)
-            a_pen(0, 0, 0)
-            q_x(0, 2)
-            a_pen(0, 0, 1)
-            a_turn(1, 0)
-            a_turn(1, 1)
-            for k in range(4):
-                q_d(0, k)
-            a_square(1, 0)
-            a_square(1, 1)
-            e2_quant(0)
+            y_gain(0, 1)
             a_mul(1, 0)
-            q_q(0, 0)
-            a_mul(1, 1)
-            e2_quant(1)
-            q_quant(0)
-            a_rsqrt(1, 0)
-            a_rsqrt(1, 1)
-            a_quant(1)
-            y_turn(1)
-            for g in range(G):
-                for k in range(4):
-                    mm2(0, g, k)
-            for k in range(4):
-                y_gain(1, k)
-            a_pen(1, 1, 0)
+            y_gain(0, 2)
             a_turn(2, 0)
-            for k in range(4):
-                r_add(0, 0, k)
-            a_pen(1, 1, 1)
-            a_turn(2, 1)
+            y_gain(0, 3)
+            q_u(0, 2)
+            q_u(0, 3)
+            a_hold(0, 1)
+            a_square(0, 1)
+            a_hold(1, 0)
+            q_x(0, 0)
+            q_d(0, 0)
+            q_x(0, 2)
+            q_d(0, 1)
+            y_turn(1)
+            a_square(1, 0)
+            a_pen_gp(0, 0)
+            a_mul(1, 1)
+            q_d(0, 2)
+            q_d(0, 3)
             a_mul(2, 0)
-            a_square(2, 0)
-            r_add(0, 1, 0)
-            r_add(0, 1, 1)
+            q_q(0, 0)
+            a_turn(2, 1)
+            q_quant(0)
+            mm2(0, 0, 0)
+            e2_copy(1, 0)
+            e2_copy(1, 1)
+            a_quant(1)
+            e2_quant(1)
+            mm2(0, 0, 1)
+            mm2(0, 0, 2)
+            mm2(0, 0, 3)
+            a_square(1, 1)
+            mm2(0, 1, 0)
+            mm2(0, 1, 1)
             a_mul(2, 1)
-            a_square(2, 1)
-            p_cast(SC, 0, 0)
-            r_add(0, 1, 2)
+            a_hold(1, 1)
+            y_gain(1, 0)
+            r_add(0, 0, 0)
+            mm2(0, 1, 2)
+            a_rsqrt(0, 1)
+            r_add(0, 0, 1)
+            mm2(0, 1, 3)
             a_quant(2)
-            r_add(0, 1, 3)
+            r_add(0, 0, 2)
+            r_add(0, 0, 3)
+            a_rsqrt(1, 0)
+            y_gain(1, 1)
             mm1(1)
-            p_cast(SC, 0, 1)
-            a_rsqrt(2, 0)
-            a_rsqrt(2, 1)
-            for nb in range(2):
-                o_turn(0, 0, nb)
-                o_copy(SC, 0, 0, nb)
-
-            q_u(1, 0)
-            q_u(1, 1)
-            q_x(1, 0)
-            p_quant(0, 0)
-            q_u(1, 2)
-            q_x(1, 1)
-            p_quant(0, 1)
-            q_u(1, 3)
-            q_x(1, 2)
-            a_pen(1, 2, 0)
-            q_x(1, 3)
-            a_pen(1, 2, 1)
-            for nb in range(2):
-                o_turn(0, 1, nb)
-                o_copy(SC, 0, 1, nb)
-                o_store(0, nb, 0, L)
+            a_square(2, 0)
+            a_pen_gp(0, 1)
+            y_gain(1, 2)
+            o_turn(0, 0, 0)
+            r_add(0, 1, 0)
+            a_hold(2, 0)
             a_turn(3, 0)
+            o_turn(0, 0, 1)
+            r_add(0, 1, 1)
+            a_square(2, 1)
+            a_rsqrt(1, 1)
+            q_u(1, 0)
+            y_gain(1, 3)
+            r_add(0, 1, 2)
+            r_add(0, 1, 3)
+            q_u(1, 1)
+            a_pen_gp(1, 0)
+            q_x(1, 0)
+            q_x(1, 1)
+            q_d(1, 0)
+            q_d(1, 1)
+            q_u(1, 2)
+            q_u(1, 3)
+            a_hold(2, 1)
             a_turn(3, 1)
-            for k in range(4):
-                q_d(1, k)
+            p_cast(SC, 0, 0)
+            q_x(1, 2)
+            p_cast(SC, 0, 1)
+            o_turn(0, 1, 0)
+            q_x(1, 3)
+            y_turn(2)
+            a_mul(3, 0)
+            o_copy(SC, 0, 0, 0)
+            q_d(1, 2)
+            q_d(1, 3)
+            o_copy(SC, 0, 0, 1)
+            a_mul(3, 1)
+            q_q(1, 0)
+            a_rsqrt(2, 0)
+            a_quant(3)
+            a_rsqrt(2, 1)
+            a_pen_gp(1, 1)
+            o_copy(SC, 0, 1, 0)
+            mm1(2)
+            q_q(1, 1)
             a_square(3, 0)
             a_square(3, 1)
-            a_mul(3, 0)
-            q_q(1, 0)
-            q_q(1, 1)
-            a_mul(3, 1)
+            a_hold(3, 0)
+            q_u(2, 0)
             q_quant(1)
+            mm2(1, 0, 0)
+            a_pen_gp(2, 0)
+            mm2(1, 0, 1)
+            y_gain(2, 0)
+            q_u(2, 1)
+            a_hold(3, 1)
             a_rsqrt(3, 0)
             a_rsqrt(3, 1)
-            y_turn(2)
-            for k in range(4):
-                y_gain(2, k)
-            a_quant(3)
-            a_pen(2, 3, 0)
-            for k in range(4):
-                mm2(1, 0, k)
-            for k in range(4):
-                r_add(1, 0, k)
-                mm2(1, 1, k)
-            p_cast(SC, 1, 0)
-            mm1(2)
-            for nb in range(4):
-                o_turn(1, 0, nb)
-                o_copy(SC, 1, 0, nb)
-            for k in range(4):
-                r_add(1, 1, k)
-
-            q_u(2, 0)
-            q_u(2, 1)
             q_u(2, 2)
-            q_x(2, 0)
             q_u(2, 3)
-            q_d(2, 0)
-            q_d(2, 1)
+            y_gain(2, 1)
+            q_x(2, 0)
+            o_turn(0, 1, 1)
+            y_gain(2, 2)
             q_x(2, 2)
-            p_cast(VC, 1, 1)
+            mm2(1, 0, 2)
+            r_add(1, 0, 0)
+            mm2(1, 0, 3)
+            r_add(1, 0, 1)
+            r_add(1, 0, 2)
+            mm2(1, 1, 0)
+            o_store(0, 0, 0, L)
+            mm2(1, 1, 1)
+            y_gain(2, 3)
+            a_pen_gp(2, 1)
+            o_copy(SC, 0, 1, 1)
+            r_add(1, 0, 3)
+            r_add(1, 1, 0)
+            p_quant(0, 0)
+            o_turn(1, 0, 0)
+            mm2(1, 1, 2)
+            q_d(2, 0)
+            r_add(1, 1, 1)
+            q_d(2, 1)
+            p_cast(SC, 1, 0)
             q_d(2, 2)
+            mm2(1, 1, 3)
             q_d(2, 3)
-            p_quant(1, 0)
+            o_copy(SC, 1, 0, 0)
+            a_pen_gp(3, 0)
+            r_add(1, 1, 2)
+            a_pen_gp(3, 1)
+            o_turn(1, 0, 1)
+            o_turn(1, 0, 2)
+            r_add(1, 1, 3)
             q_q(2, 0)
-            p_quant(1, 1)
+            o_turn(1, 0, 3)
+            o_store(0, 1, 0, L)
+            o_turn(1, 1, 0)
+            p_quant(0, 1)
+            p_quant(1, 0)
+            o_copy(SC, 1, 0, 1)
+            o_turn(1, 1, 1)
+            o_copy(SC, 1, 0, 2)
             q_quant(2)
-            store_scales(0, 768)
-            for nb in range(4):
-                o_turn(1, 1, nb)
-                o_copy(SC, 1, 1, nb)
-                o_store(1, nb, 0, L)
-            a_pen(2, 3, 1)
-            for g in range(G):
-                for k in range(4):
-                    mm2(2, g, k)
-            for k in range(4):
-                r_add(2, 0, k)
+            o_turn(1, 1, 2)
+            o_copy(SC, 1, 0, 3)
+            mm2(2, 0, 0)
+            mm2(2, 0, 1)
+            o_copy(SC, 1, 1, 0)
+            mm2(2, 0, 2)
+            mm2(2, 0, 3)
+            p_cast(VC, 1, 1)
+            mm2(2, 1, 0)
+            r_add(2, 0, 0)
+            mm2(2, 1, 1)
+            r_add(2, 0, 1)
+            mm2(2, 1, 2)
+            r_add(2, 0, 2)
+            o_copy(SC, 1, 1, 1)
+            o_store(1, 0, 0, L)
+            o_turn(1, 1, 3)
+            o_copy(SC, 1, 1, 2)
+            mm2(2, 1, 3)
+            o_store(1, 1, 0, L)
+            o_store(1, 2, 0, L)
+            r_add(2, 0, 3)
+            p_quant(1, 1)
             r_add(2, 1, 0)
-            p_cast(VC, 2, 0)
-            for nb in range(2):
-                o_turn(2, 0, nb)
-                o_copy(SC, 2, 0, nb)
-                o_store(2, nb, 0, 512)
             r_add(2, 1, 1)
+            o_copy(SC, 1, 1, 3)
+            store_scales(0, 768)
+            o_turn(2, 0, 0)
+            o_copy(SC, 2, 0, 0)
             r_add(2, 1, 2)
-            p_quant(2, 0)
             r_add(2, 1, 3)
-            for nb in range(2):
-                o_turn(2, 1, nb)
+            p_cast(VC, 2, 0)
+            o_store(1, 3, 0, L)
+            o_turn(2, 0, 1)
+            o_store(2, 0, 0, 512)
+            o_copy(VC, 2, 0, 1)
+            o_turn(2, 1, 0)
+            o_turn(2, 1, 1)
+            p_cast(SC, 2, 1)
+            o_store(2, 1, 0, 512)
             o_copy(SC, 2, 1, 0)
-            o_store(2, 0, 512, L)
-            o_copy(VC, 2, 1, 1)
-            o_store(2, 1, 512, L)
-            p_cast(VC, 2, 1)
+            p_quant(2, 0)
             p_quant(2, 1)
+            o_copy(VC, 2, 1, 1)
+            o_store(2, 0, 512, L)
             store_scales(768, N)
+            o_store(2, 1, 512, L)

@@ -54,7 +54,7 @@ def tile_polynomialpostnonlinearlibraryunmixinggr_x1_kernel(
         e2_in = [work.tile([P, 2048], BF16, align_bytes=64, tag="e_in", name="e2_in%d" % g) for g in range(G)]
         p_scales = keep.tile([P, G, N], U8, align_bytes=64, name="p_scales")
 
-        at, a_t, ap_in, ap_codes, ap_scales, pen = {}, {}, {}, {}, {}, {}
+        at, sq, ap_in, ap_codes, ap_scales, pen = {}, {}, {}, {}, {}, {}
         yt, yr, m1, u2, xx, q_in, q_codes, q_scales = {}, {}, {}, {}, {}, {}, {}, {}
         h2, res, p_in, o_sb, o_ps, e2_ps = {}, {}, {}, {}, {}, {}
 
@@ -142,33 +142,25 @@ def tile_polynomialpostnonlinearlibraryunmixinggr_x1_kernel(
             c = [i for i, (n0, n) in enumerate(CHUNKS) if n0 <= B * s < n0 + n][0]
             n0, n = CHUNKS[c]
             if (c, g) not in pen:
-                pen[c, g] = work.tile([P, 2, n, 2], F32, tag="pen%d" % g, name="pen")
-            r = s - n0 // B
-            return pen[c, g][:, :, B * r : B * r + B, :].rearrange("p u n d -> p u (n d)")
-
-        def a_hold(s, g):
-            if s not in a_t:
-                a_t[s] = work.tile([P, G, 2, B], F32, align_bytes=64, tag="a_t", name="a_t")
-            S.copy(out=a_t[s][:, g], in_=at[s, g][:])
+                pen[c, g] = work.tile([P, 4, n], F32, tag="pen%d" % g, name="pen")
+            return pen[c, g][:, :, B * s - n0 : B * s - n0 + B]
 
         def a_square(s, g):
-            S.activation(out=pen_part(s, g), in_=raw_t(s, g), func=ACT.Square)
+            if (s, g) not in sq:
+                sq[s, g] = work.tile([P, 2, 2 * B], F32, tag="sq", name="sq")
+            S.activation(out=sq[s, g][:], in_=raw_t(s, g), func=ACT.Square)
 
         def a_rsqrt(s, g):
-            t = pen_part(s, g)
+            t = sq[s, g][:]
             S.activation(out=t, in_=t, func=ACT.Abs_reciprocal_sqrt, scale=1.0 / 0.09, bias=0.01 / 0.09)
 
         def a_pen(s, g):
-            t = pen_part(s, g)
-            V.tensor_tensor(out=t, in0=raw_t(s, g), in1=t, op=ALU.mult)
-
-        def a_pen_gp(s, g):
-            t = pen_part(s, g)
-            src = a_t[s][:, g].bitcast(BF16)
-            for u in range(2):
-                for h in range(2):
-                    w = slice(B * h, B * h + B)
-                    GP.tensor_tensor(out=t[:, u, w], in0=src[:, u, w], in1=t[:, u, w], op=ALU.mult)
+            V.tensor_tensor(
+                out=pen_part(s, g).rearrange("p (u d) n -> p u n d", d=2),
+                in0=raw_t(s, g).rearrange("p u (n d) -> p u n d", d=2),
+                in1=sq[s, g][:].rearrange("p u (n d) -> p u n d", d=2),
+                op=ALU.mult,
+            )
 
         def y_turn(c):
             n0, n = CHUNKS[c]
@@ -250,17 +242,20 @@ def tile_polynomialpostnonlinearlibraryunmixinggr_x1_kernel(
                 op1=ALU.subtract,
             )
 
+        def q_slope(c, h):
+            t = u2[c][:, 2 * h : 2 * h + 2, :]
+            S.activation(out=t, in_=t, func=ACT.Copy, bias=1.0)
+
         def q_q(c, r):
             n0, n = CHUNKS[c]
             if c not in q_in:
                 q_in[c] = work.tile([P, n, 4], BF16, align_bytes=64, tag="q_in", name="q_in")
-            V.scalar_tensor_tensor(
-                out=q_in[c][:, B * r : B * r + B, :],
-                in0=u2[c][:, :, B * r : B * r + B].rearrange("p t n -> p n t"),
-                scalar=1.0,
-                in1=xx[c][:, :, B * r : B * r + B].rearrange("p t n -> p n t"),
-                op0=ALU.add,
-                op1=ALU.mult,
+            w = slice(B * r, B * r + B)
+            V.tensor_tensor(
+                out=q_in[c][:, w, :].rearrange("p (n i) t -> p n t i", i=4),
+                in0=u2[c][:, :, w].rearrange("p t (n i) -> p n t i", i=4),
+                in1=xx[c][:, :, w].rearrange("p t (n i) -> p n t i", i=4),
+                op=ALU.mult,
             )
 
         def q_quant(c):
@@ -296,7 +291,7 @@ def tile_polynomialpostnonlinearlibraryunmixinggr_x1_kernel(
                 out=res[c, g][:, k, :],
                 in0=h2[c, g, k // (512 // n)][:, k % (512 // n), :],
                 scalar=psi4[:, g, k : k + 1],
-                in1=pen[c, g][:, k // 2, :, k % 2],
+                in1=pen[c, g][:, k, :],
                 op0=ALU.mult,
                 op1=ALU.add,
             )
@@ -338,7 +333,7 @@ def tile_polynomialpostnonlinearlibraryunmixinggr_x1_kernel(
 
         def o_copy(copy, c, g, nb):
             if (c, nb) not in o_sb:
-                o_sb[c, nb] = work.tile([P, L], F32, tag="o_sb", bufs=6, name="o_sb")
+                o_sb[c, nb] = work.tile([P, L], F32, tag="o_sb", bufs=5, name="o_sb")
             copy(
                 out=o_sb[c, nb][:, 512 * g : 512 * g + 512].rearrange("n (p t) -> n p t", t=4),
                 in_=o_ps[c, g, nb][:].rearrange("n t p -> n p t"),
@@ -369,233 +364,231 @@ def tile_polynomialpostnonlinearlibraryunmixinggr_x1_kernel(
             GP.tensor_tensor(out=rho_s[:], in0=rho4[:], in1=rho4[:], op=ALU.mult)
             GP.tensor_scalar(out=rho_h[:], in0=rho_s[:], scalar1=0.5, scalar2=0.0, op0=ALU.mult, op1=ALU.add)
 
-            e1_part(VC, 0, 0, 96)
+            e1_part(SC, 0, 80, 128)
             b_spread()
+            e1_part(VC, 0, 0, 80)
             e2_turn(0, 0)
-            e1_part(SC, 0, 96, 128)
-            e2_copy(0, 0)
-            e1_quant(0)
             a_turn(0, 0)
-            e2_turn(0, 1)
+            e1_quant(0)
             a_turn(0, 1)
-            y_turn(0)
             a_mul(0, 0)
-            e1_part(VC, 1, 0, 96)
-            e1_part(SC, 1, 96, 128)
+            e2_turn(0, 1)
+            e1_part(VC, 1, 0, 80)
+            a_mul(0, 1)
+            e2_copy(0, 0)
+            e1_part(SC, 1, 80, 128)
             e1_quant(1)
-            a_turn(1, 0)
-            a_hold(0, 0)
+            a_quant(0)
             a_square(0, 0)
             e2_copy(0, 1)
-            a_mul(0, 1)
-            a_quant(0)
-            mm1(0)
-            e2_turn(1, 0)
-            a_turn(1, 1)
-            a_rsqrt(0, 0)
             e2_quant(0)
+            a_rsqrt(0, 0)
+            a_square(0, 1)
+            y_turn(0)
             y_gain(0, 0)
-            e2_turn(1, 1)
+            mm1(0)
+            y_gain(0, 1)
+            y_gain(0, 2)
+            a_turn(1, 0)
+            a_rsqrt(0, 1)
+            a_pen(0, 0)
             q_u(0, 0)
             q_u(0, 1)
-            y_gain(0, 1)
-            a_mul(1, 0)
-            y_gain(0, 2)
-            a_turn(2, 0)
-            y_gain(0, 3)
+            e2_turn(1, 0)
+            q_x(0, 0)
+            a_square(1, 0)
             q_u(0, 2)
             q_u(0, 3)
-            a_hold(0, 1)
-            a_square(0, 1)
-            a_hold(1, 0)
-            q_x(0, 0)
             q_d(0, 0)
+            y_gain(0, 3)
+            a_rsqrt(1, 0)
             q_x(0, 2)
+            a_pen(0, 1)
+            q_slope(0, 0)
             q_d(0, 1)
-            y_turn(1)
-            a_square(1, 0)
-            a_pen_gp(0, 0)
-            a_mul(1, 1)
-            q_d(0, 2)
-            q_d(0, 3)
-            a_mul(2, 0)
-            q_q(0, 0)
-            a_turn(2, 1)
-            q_quant(0)
-            mm2(0, 0, 0)
             e2_copy(1, 0)
-            e2_copy(1, 1)
-            a_quant(1)
-            e2_quant(1)
-            mm2(0, 0, 1)
-            mm2(0, 0, 2)
-            mm2(0, 0, 3)
+            q_d(0, 2)
+            q_slope(0, 1)
+            e2_turn(1, 1)
+            a_turn(1, 1)
+            q_d(0, 3)
             a_square(1, 1)
+            a_mul(1, 0)
+            e2_copy(1, 1)
+            a_turn(2, 0)
+            a_pen(1, 0)
+            q_q(0, 0)
+            a_rsqrt(1, 1)
+            a_mul(1, 1)
+            q_quant(0)
+            a_quant(1)
+            y_turn(1)
+            mm2(0, 0, 0)
+            mm2(0, 0, 1)
+            a_pen(1, 1)
+            e2_quant(1)
+            mm2(0, 0, 2)
+            a_turn(2, 1)
+            mm2(0, 0, 3)
             mm2(0, 1, 0)
+            a_square(2, 0)
             mm2(0, 1, 1)
-            a_mul(2, 1)
-            a_hold(1, 1)
-            y_gain(1, 0)
+            a_rsqrt(2, 0)
             r_add(0, 0, 0)
-            mm2(0, 1, 2)
-            a_rsqrt(0, 1)
+            a_mul(2, 0)
+            y_gain(1, 0)
             r_add(0, 0, 1)
-            mm2(0, 1, 3)
+            mm2(0, 1, 2)
+            a_mul(2, 1)
+            a_pen(2, 0)
             a_quant(2)
             r_add(0, 0, 2)
-            r_add(0, 0, 3)
-            a_rsqrt(1, 0)
-            y_gain(1, 1)
+            a_square(2, 1)
+            mm2(0, 1, 3)
             mm1(1)
-            a_square(2, 0)
-            a_pen_gp(0, 1)
-            y_gain(1, 2)
+            r_add(0, 0, 3)
+            a_rsqrt(2, 1)
             o_turn(0, 0, 0)
             r_add(0, 1, 0)
-            a_hold(2, 0)
-            a_turn(3, 0)
-            o_turn(0, 0, 1)
             r_add(0, 1, 1)
-            a_square(2, 1)
-            a_rsqrt(1, 1)
             q_u(1, 0)
-            y_gain(1, 3)
+            y_gain(1, 1)
             r_add(0, 1, 2)
             r_add(0, 1, 3)
-            q_u(1, 1)
-            a_pen_gp(1, 0)
+            a_pen(2, 1)
             q_x(1, 0)
-            q_x(1, 1)
-            q_d(1, 0)
-            q_d(1, 1)
+            q_u(1, 1)
+            o_turn(0, 0, 1)
+            y_gain(1, 2)
+            y_gain(1, 3)
+            a_turn(3, 0)
             q_u(1, 2)
-            q_u(1, 3)
-            a_hold(2, 1)
-            a_turn(3, 1)
-            p_cast(SC, 0, 0)
-            q_x(1, 2)
-            p_cast(SC, 0, 1)
             o_turn(0, 1, 0)
+            q_x(1, 1)
+            p_cast(SC, 0, 0)
+            o_copy(SC, 0, 0, 0)
+            q_u(1, 3)
+            q_x(1, 2)
+            o_turn(0, 1, 1)
+            a_turn(3, 1)
+            q_d(1, 0)
             q_x(1, 3)
+            q_d(1, 1)
+            o_copy(SC, 0, 0, 1)
+            q_slope(1, 0)
+            q_d(1, 2)
             y_turn(2)
             a_mul(3, 0)
-            o_copy(SC, 0, 0, 0)
-            q_d(1, 2)
-            q_d(1, 3)
-            o_copy(SC, 0, 0, 1)
             a_mul(3, 1)
-            q_q(1, 0)
-            a_rsqrt(2, 0)
-            a_quant(3)
-            a_rsqrt(2, 1)
-            a_pen_gp(1, 1)
             o_copy(SC, 0, 1, 0)
-            mm1(2)
+            q_slope(1, 1)
+            q_d(1, 3)
+            o_store(0, 0, 0, L)
+            a_quant(3)
+            o_copy(SC, 0, 1, 1)
+            q_q(1, 0)
             q_q(1, 1)
-            a_square(3, 0)
-            a_square(3, 1)
-            a_hold(3, 0)
+            mm1(2)
             q_u(2, 0)
-            q_quant(1)
-            mm2(1, 0, 0)
-            a_pen_gp(2, 0)
-            mm2(1, 0, 1)
-            y_gain(2, 0)
             q_u(2, 1)
-            a_hold(3, 1)
-            a_rsqrt(3, 0)
-            a_rsqrt(3, 1)
+            q_quant(1)
             q_u(2, 2)
             q_u(2, 3)
-            y_gain(2, 1)
             q_x(2, 0)
-            o_turn(0, 1, 1)
-            y_gain(2, 2)
+            a_square(3, 0)
+            mm2(1, 0, 0)
+            p_cast(SC, 0, 1)
             q_x(2, 2)
-            mm2(1, 0, 2)
             r_add(1, 0, 0)
+            mm2(1, 0, 1)
+            y_gain(2, 0)
+            y_gain(2, 1)
+            mm2(1, 0, 2)
             mm2(1, 0, 3)
             r_add(1, 0, 1)
+            y_gain(2, 2)
+            a_rsqrt(3, 0)
             r_add(1, 0, 2)
             mm2(1, 1, 0)
-            o_store(0, 0, 0, L)
             mm2(1, 1, 1)
             y_gain(2, 3)
-            a_pen_gp(2, 1)
-            o_copy(SC, 0, 1, 1)
+            mm2(1, 1, 2)
+            o_store(0, 1, 0, L)
+            mm2(1, 1, 3)
             r_add(1, 0, 3)
             r_add(1, 1, 0)
-            p_quant(0, 0)
-            o_turn(1, 0, 0)
-            mm2(1, 1, 2)
             q_d(2, 0)
-            r_add(1, 1, 1)
+            q_slope(2, 0)
+            o_turn(1, 0, 0)
+            a_square(3, 1)
+            q_slope(2, 1)
             q_d(2, 1)
-            p_cast(SC, 1, 0)
+            r_add(1, 1, 1)
             q_d(2, 2)
-            mm2(1, 1, 3)
-            q_d(2, 3)
+            a_rsqrt(3, 1)
             o_copy(SC, 1, 0, 0)
-            a_pen_gp(3, 0)
             r_add(1, 1, 2)
-            a_pen_gp(3, 1)
             o_turn(1, 0, 1)
-            o_turn(1, 0, 2)
+            q_d(2, 3)
             r_add(1, 1, 3)
-            q_q(2, 0)
+            p_cast(VC, 1, 0)
+            o_turn(1, 0, 2)
             o_turn(1, 0, 3)
-            o_store(0, 1, 0, L)
-            o_turn(1, 1, 0)
-            p_quant(0, 1)
-            p_quant(1, 0)
+            p_quant(0, 0)
             o_copy(SC, 1, 0, 1)
-            o_turn(1, 1, 1)
+            q_q(2, 0)
             o_copy(SC, 1, 0, 2)
-            q_quant(2)
+            a_pen(3, 0)
+            o_turn(1, 1, 0)
+            o_turn(1, 1, 1)
             o_turn(1, 1, 2)
-            o_copy(SC, 1, 0, 3)
-            mm2(2, 0, 0)
-            mm2(2, 0, 1)
-            o_copy(SC, 1, 1, 0)
-            mm2(2, 0, 2)
-            mm2(2, 0, 3)
-            p_cast(VC, 1, 1)
-            mm2(2, 1, 0)
-            r_add(2, 0, 0)
-            mm2(2, 1, 1)
-            r_add(2, 0, 1)
-            mm2(2, 1, 2)
-            r_add(2, 0, 2)
-            o_copy(SC, 1, 1, 1)
-            o_store(1, 0, 0, L)
             o_turn(1, 1, 3)
+            o_copy(SC, 1, 0, 3)
+            q_quant(2)
+            o_copy(SC, 1, 1, 0)
+            mm2(2, 0, 0)
+            o_store(1, 0, 0, L)
+            mm2(2, 0, 1)
+            o_copy(SC, 1, 1, 1)
             o_copy(SC, 1, 1, 2)
-            mm2(2, 1, 3)
             o_store(1, 1, 0, L)
-            o_store(1, 2, 0, L)
-            r_add(2, 0, 3)
-            p_quant(1, 1)
-            r_add(2, 1, 0)
-            r_add(2, 1, 1)
+            a_pen(3, 1)
+            mm2(2, 0, 2)
             o_copy(SC, 1, 1, 3)
-            store_scales(0, 768)
-            o_turn(2, 0, 0)
-            o_copy(SC, 2, 0, 0)
-            r_add(2, 1, 2)
-            r_add(2, 1, 3)
-            p_cast(VC, 2, 0)
+            o_store(1, 2, 0, L)
+            mm2(2, 0, 3)
             o_store(1, 3, 0, L)
+            r_add(2, 0, 0)
+            mm2(2, 1, 0)
+            p_quant(0, 1)
+            p_cast(SC, 1, 1)
+            r_add(2, 0, 1)
+            mm2(2, 1, 1)
+            r_add(2, 0, 2)
+            r_add(2, 0, 3)
+            p_quant(1, 0)
+            mm2(2, 1, 2)
+            mm2(2, 1, 3)
+            p_quant(1, 1)
+            o_turn(2, 0, 0)
+            p_cast(SC, 2, 0)
+            r_add(2, 1, 0)
+            o_copy(SC, 2, 0, 0)
+            r_add(2, 1, 1)
             o_turn(2, 0, 1)
+            o_copy(SC, 2, 0, 1)
+            r_add(2, 1, 2)
             o_store(2, 0, 0, 512)
-            o_copy(VC, 2, 0, 1)
+            store_scales(0, 768)
+            r_add(2, 1, 3)
+            o_store(2, 1, 0, 512)
             o_turn(2, 1, 0)
             o_turn(2, 1, 1)
-            p_cast(SC, 2, 1)
-            o_store(2, 1, 0, 512)
             o_copy(SC, 2, 1, 0)
+            o_copy(SC, 2, 1, 1)
             p_quant(2, 0)
-            p_quant(2, 1)
-            o_copy(VC, 2, 1, 1)
+            p_cast(VC, 2, 1)
             o_store(2, 0, 512, L)
-            store_scales(768, N)
+            p_quant(2, 1)
             o_store(2, 1, 512, L)
+            store_scales(768, N)

from contextlib import ExitStack

import concourse.mybir as mybir
from concourse.masks import make_identity

N, L, K = 1024, 1024, 512
FLOPS = 2 * 2 * N * L * K

F32 = mybir.dt.float32
BF16 = mybir.dt.bfloat16
U32 = mybir.dt.uint32
I32 = mybir.dt.int32
U8 = mybir.dt.uint8
X4 = mybir.dt.float8_e4m3fn_x4
ACT = mybir.ActivationFunctionType
ALU = mybir.AluOpType

P = 128
G = L // 512
B = 256
CHUNKS = ((0, 256), (256, 512), (768, 256))


def tile_polynomialpostnonlinearlibraryunmixinggr_x1_kernel(
    tc, y, a, e, psi, rho, b, out_0, out_1, out_2
):
    nc = tc.nc
    V, S, T, GP = nc.vector, nc.scalar, nc.tensor, nc.gpsimd
    with ExitStack() as ctx:
        keep = ctx.enter_context(tc.tile_pool(name="keep", bufs=1))
        one = ctx.enter_context(tc.tile_pool(name="one", bufs=1))
        work = ctx.enter_context(tc.tile_pool(name="work", bufs=2))
        psum = ctx.enter_context(tc.psum_pool(name="psum", bufs=2))

        e_raw = [keep.tile([P, 4, K], BF16, name="e_raw%d" % g) for g in range(G)]
        a_raw = [keep.tile([P, 2, L], BF16, name="a_raw%d" % s) for s in range(4)]
        y_raw = [keep.tile([P, 2, K], BF16, name="y_raw%d" % s) for s in range(4)]
        b_col = keep.tile([P, 8], BF16, name="b_col")
        psi4 = keep.tile([P, G, 4], BF16, name="psi4")
        rho4 = keep.tile([P, 4], BF16, name="rho4")
        ident = keep.tile([P, P], F32, name="ident")
        ident_bf = keep.tile([P, P], BF16, name="ident_bf")
        warm = keep.tile([P, 1], F32, name="warm")
        rho_f = keep.tile([P, 4], F32, name="rho_f")
        rho_2 = keep.tile([P, 4], F32, name="rho_2")
        rho_s = keep.tile([P, 4], F32, name="rho_s")
        rho_h = keep.tile([P, 4], F32, name="rho_h")
        b_all = keep.tile([P, N], BF16, name="b_all")
        e1_codes = keep.tile([P, G, 512], U32, align_bytes=64, name="e1_codes")
        e1_scales = keep.tile([P, G, 512], U8, align_bytes=64, name="e1_scales")
        e2_codes = keep.tile([P, G, 512], U32, align_bytes=64, name="e2_codes")
        e2_scales = keep.tile([P, G, 512], U8, align_bytes=64, name="e2_scales")
        e1_in = [work.tile([P, 2048], BF16, align_bytes=64, tag="e_in", name="e1_in%d" % g) for g in range(G)]
        e2_in = [work.tile([P, 2048], BF16, align_bytes=64, tag="e_in", name="e2_in%d" % g) for g in range(G)]
        p_scales = keep.tile([P, G, N], U8, align_bytes=64, name="p_scales")

        at, sq, ap_in, ap_codes, ap_scales, pen = {}, {}, {}, {}, {}, {}
        yt, yr, m1, u2, xx, q_in, q_codes, q_scales = {}, {}, {}, {}, {}, {}, {}, {}
        h2, res, p_in, o_sb, o_ps, e2_ps = {}, {}, {}, {}, {}, {}

        def load_e(g):
            nc.sync.dma_start(
                out=e_raw[g][:], in_=e[512 * g : 512 * g + 512, :].rearrange("(p j) k -> p j k", j=4)
            )

        def load_a(s):
            nc.sync.dma_start(
                out=a_raw[s][:], in_=a[B * s : B * s + B, :].rearrange("(r p) l -> p r l", p=P)
            )

        def load_y(s):
            nc.sync.dma_start(
                out=y_raw[s][:], in_=y[B * s : B * s + B, :].rearrange("(r p) k -> p r k", p=P)
            )

        def b_spread():
            bp = psum.tile([P, 8, P], BF16, tag="tp", name="bp")
            for i in range(8):
                T.transpose(bp[:, i, :], b_col[:, i : i + 1].to_broadcast([P, P]), ident_bf[:])
            S.copy(out=b_all[:].rearrange("x (p i) -> x p i", i=8), in_=bp[:].rearrange("x i p -> x p i"))

        def e1_part(copy, g, m0, m1_):
            copy(
                out=e1_in[g][:].rearrange("p (t m j) -> p t m j", t=4, j=4)[:, :, m0:m1_],
                in_=e_raw[g][:].rearrange("p j (m t) -> p t m j", t=4)[:, :, m0:m1_],
            )

        def e1_quant(g):
            V.quantize_mx(out=e1_codes[:, g, :].bitcast(X4), scales=e1_scales[:, g, :], in_=e1_in[g][:])

        def e2_turn(g, h):
            ep = psum.tile([P, 2, 2, P], F32, tag="tp", name="ep")
            for i in range(2):
                words = e_raw[g][:, 2 * h + i, :].bitcast(F32)
                for u in range(2):
                    T.transpose(ep[:, i, u, :], words[:, u:256:2], ident[:])
            e2_ps[g, h] = ep

        def e2_copy(g, h):
            ep = e2_ps[g, h]
            S.copy(
                out=e2_in[g][:].bitcast(F32).rearrange("p (i m u) -> p i m u", i=4, u=2)[:, 2 * h : 2 * h + 2],
                in_=ep[:].rearrange("p i u m -> p i m u"),
            )

        def e2_quant(g):
            V.quantize_mx(out=e2_codes[:, g, :].bitcast(X4), scales=e2_scales[:, g, :], in_=e2_in[g][:])

        def a_turn(s, g):
            t = psum.tile([P, 2, B], F32, tag="at", name="at")
            at[s, g] = t
            for r in range(2):
                words = a_raw[s][:, r, :].bitcast(F32)
                for u in range(2):
                    T.transpose(
                        t[:, u, P * r : P * r + P], words[:, 256 * g + u : 256 * g + 256 : 2], ident[:]
                    )

        def a_mul(s, g):
            if s not in ap_in:
                ap_in[s] = work.tile([P, G, B, 4], BF16, align_bytes=64, tag="ap_in", name="ap_in")
            V.tensor_tensor(
                out=ap_in[s][:, g].rearrange("p n (u d) -> p n u d", u=2),
                in0=at[s, g][:].bitcast(BF16).rearrange("p u (n d) -> p n u d", d=2),
                in1=psi4[:, g, :].rearrange("p (o u d) -> p o u d", o=1, u=2).to_broadcast([P, B, 2, 2]),
                op=ALU.mult,
            )

        def a_quant(s):
            ap_codes[s] = work.tile([P, G, B], U32, align_bytes=64, tag="ap_codes", name="ap_codes")
            ap_scales[s] = work.tile([P, G, B], U8, align_bytes=64, tag="ap_scales", name="ap_scales")
            V.quantize_mx(
                out=ap_codes[s][:].rearrange("p g n -> p (g n)").bitcast(X4),
                scales=ap_scales[s][:].rearrange("p g n -> p (g n)"),
                in_=ap_in[s][:].rearrange("p g n t -> p (g n t)"),
            )

        def raw_t(s, g):
            return at[s, g][:].bitcast(BF16)

        def pen_part(s, g):
            c = [i for i, (n0, n) in enumerate(CHUNKS) if n0 <= B * s < n0 + n][0]
            n0, n = CHUNKS[c]
            if (c, g) not in pen:
                pen[c, g] = work.tile([P, 4, n], F32, tag="pen%d" % g, name="pen")
            return pen[c, g][:, :, B * s - n0 : B * s - n0 + B]

        def a_square(s, g):
            if (s, g) not in sq:
                sq[s, g] = work.tile([P, 2, 2 * B], F32, tag="sq", name="sq")
            S.activation(out=sq[s, g][:], in_=raw_t(s, g), func=ACT.Square)

        def a_rsqrt(s, g):
            t = sq[s, g][:]
            S.activation(out=t, in_=t, func=ACT.Abs_reciprocal_sqrt, scale=1.0 / 0.09, bias=0.01 / 0.09)

        def a_pen(s, g):
            V.tensor_tensor(
                out=pen_part(s, g).rearrange("p (u d) n -> p u n d", d=2),
                in0=raw_t(s, g).rearrange("p u (n d) -> p u n d", d=2),
                in1=sq[s, g][:].rearrange("p u (n d) -> p u n d", d=2),
                op=ALU.mult,
            )

        def y_turn(c):
            n0, n = CHUNKS[c]
            per = 512 // n
            for u in range(2):
                if u % per == 0:
                    ps = psum.tile([P, per, n], F32, tag="tp", name="yt")
                yt[c, u] = ps
                for r in range(n // P):
                    row = n0 // P + r
                    words = y_raw[row // 2][:, row % 2, :].bitcast(F32)
                    T.transpose(ps[:, u % per, P * r : P * r + P], words[:, u:256:2], ident[:])

        def y_gain(c, k):
            n0, n = CHUNKS[c]
            if c not in yr:
                yr[c] = one.tile([P, 4, n], F32, tag="yr", name="yr")
            u, d = k // 2, k % 2
            src = yt[c, u][:].bitcast(BF16).rearrange("p u (n d) -> p u d n", d=2)
            S.activation(
                out=yr[c][:, k, :], in_=src[:, u % (512 // n), d, :], func=ACT.Copy, scale=rho_f[:, k : k + 1]
            )

        def mm1(c):
            n0, n = CHUNKS[c]
            per = 512 // n
            for k in range(4):
                if k % per == 0:
                    t = psum.tile([P, per, n], F32, tag="mm", bufs=4, name="m1")
                m1[c, k] = t
                for r in range(n // B):
                    s = n0 // B + r
                    for g in range(G):
                        T.matmul_mx(
                            out=t[:, k % per, B * r : B * r + B],
                            lhsT=e1_codes[:, g, P * k : P * k + P].bitcast(X4),
                            lhsT_scale=e1_scales[:, g, P * k : P * k + P],
                            rhs=ap_codes[s][:, g, :].bitcast(X4),
                            rhs_scale=ap_scales[s][:, g, :],
                            start=(g == 0),
                            stop=(g == G - 1),
                        )

        def q_u(c, k):
            n0, n = CHUNKS[c]
            if c not in u2:
                u2[c] = work.tile([P, 4, n], F32, tag="u2", name="u2")
            V.scalar_tensor_tensor(
                out=u2[c][:, k, :],
                in0=m1[c, k][:, k % (512 // n), :],
                scalar=rho_2[:, k : k + 1],
                in1=b_all[:, n0 : n0 + n],
                op0=ALU.mult,
                op1=ALU.mult,
            )

        def q_x(c, k):
            n0, n = CHUNKS[c]
            per = 512 // n
            if c not in xx:
                xx[c] = one.tile([P, 4, n], F32, tag="xx", name="xx")
            V.scalar_tensor_tensor(
                out=xx[c][:, k : k + per, :],
                in0=u2[c][:, k : k + per, :],
                scalar=2.0,
                in1=m1[c, k][:],
                op0=ALU.add,
                op1=ALU.mult,
            )

        def q_d(c, k):
            n0, n = CHUNKS[c]
            V.scalar_tensor_tensor(
                out=xx[c][:, k, :],
                in0=xx[c][:, k, :],
                scalar=rho_h[:, k : k + 1],
                in1=yr[c][:, k, :],
                op0=ALU.mult,
                op1=ALU.subtract,
            )

        def q_slope(c, h):
            t = u2[c][:, 2 * h : 2 * h + 2, :]
            S.activation(out=t, in_=t, func=ACT.Copy, bias=1.0)

        def q_q(c, r):
            n0, n = CHUNKS[c]
            if c not in q_in:
                q_in[c] = work.tile([P, n, 4], BF16, align_bytes=64, tag="q_in", name="q_in")
            w = slice(B * r, B * r + B)
            V.tensor_tensor(
                out=q_in[c][:, w, :].rearrange("p (n i) t -> p n t i", i=4),
                in0=u2[c][:, :, w].rearrange("p t (n i) -> p n t i", i=4),
                in1=xx[c][:, :, w].rearrange("p t (n i) -> p n t i", i=4),
                op=ALU.mult,
            )

        def q_quant(c):
            n0, n = CHUNKS[c]
            q_codes[c] = work.tile([P, n], U32, align_bytes=64, tag="q_codes", name="q_codes")
            q_scales[c] = work.tile([P, n], U8, align_bytes=64, tag="q_scales", name="q_scales")
            V.quantize_mx(
                out=q_codes[c][:].bitcast(X4),
                scales=q_scales[c][:],
                in_=q_in[c][:].rearrange("p n t -> p (n t)"),
            )

        def mm2(c, g, k):
            n0, n = CHUNKS[c]
            per = 512 // n
            if (c, g, k // per) not in h2:
                h2[c, g, k // per] = psum.tile([P, per, n], F32, tag="mm", bufs=4, name="h2")
            T.matmul_mx(
                out=h2[c, g, k // per][:, k % per, :],
                lhsT=e2_codes[:, g, P * k : P * k + P].bitcast(X4),
                lhsT_scale=e2_scales[:, g, P * k : P * k + P],
                rhs=q_codes[c][:].bitcast(X4),
                rhs_scale=q_scales[c][:],
                start=True,
                stop=True,
            )

        def r_add(c, g, k):
            n0, n = CHUNKS[c]
            if (c, g) not in res:
                res[c, g] = work.tile([P, 4, n], F32, tag="res%d" % g, name="res")
            V.scalar_tensor_tensor(
                out=res[c, g][:, k, :],
                in0=h2[c, g, k // (512 // n)][:, k % (512 // n), :],
                scalar=psi4[:, g, k : k + 1],
                in1=pen[c, g][:, k, :],
                op0=ALU.mult,
                op1=ALU.add,
            )

        def p_cast(copy, c, g):
            n0, n = CHUNKS[c]
            t = work.tile([P, n, 4], BF16, align_bytes=64, tag="p_in%d" % g, name="p_in")
            p_in[c, g] = t
            copy(
                out=t[:].rearrange("p (n i) t -> p n t i", i=4),
                in_=res[c, g][:].rearrange("p t (n i) -> p n t i", i=4),
            )

        def p_quant(c, g):
            n0, n = CHUNKS[c]
            codes = work.tile([P, n], U32, align_bytes=64, tag="p_codes%d" % g, name="p_codes")
            V.quantize_mx(
                out=codes[:].bitcast(X4),
                scales=p_scales[:, g, n0 : n0 + n],
                in_=p_in[c, g][:].rearrange("p n t -> p (n t)"),
            )
            nc.sync.dma_start(
                out=out_1[g, :, n0 : n0 + n, :].rearrange("p m t -> p (m t)").bitcast(I32),
                in_=codes[:].bitcast(I32),
            )

        def store_scales(n0, n1):
            for s in range(4):
                nc.sync.dma_start(
                    out=out_2[:, 4 * s : 4 * s + 4, n0:n1].rearrange("g q m -> q g m").bitcast(I32),
                    in_=p_scales[32 * s : 32 * s + 4, :, n0:n1].bitcast(I32),
                )

        def o_turn(c, g, nb):
            t = psum.tile([P, 4, P], F32, tag="tp", name="ot")
            o_ps[c, g, nb] = t
            for k in range(4):
                T.transpose(t[:, k, :], res[c, g][:, k, P * nb : P * nb + P], ident[:])

        def o_copy(copy, c, g, nb):
            if (c, nb) not in o_sb:
                o_sb[c, nb] = work.tile([P, L], F32, tag="o_sb", bufs=5, name="o_sb")
            copy(
                out=o_sb[c, nb][:, 512 * g : 512 * g + 512].rearrange("n (p t) -> n p t", t=4),
                in_=o_ps[c, g, nb][:].rearrange("n t p -> n p t"),
            )

        def o_store(c, nb, l0, l1):
            r0 = CHUNKS[c][0] + P * nb
            nc.sync.dma_start(out=out_0[r0 : r0 + P, l0:l1], in_=o_sb[c, nb][:, l0:l1])

        make_identity(nc, ident_bf[:])
        make_identity(nc, ident[:])
        VC, SC = V.tensor_copy, S.copy
        with tc.manual_schedule():
            S.dma_start(out=b_col[:], in_=b.rearrange("(p i) -> p i", i=8))
            S.dma_start(out=psi4[:], in_=psi.rearrange("(g p t) -> p g t", g=G, t=4))
            S.dma_start(out=rho4[:], in_=rho.rearrange("(p t) -> p t", t=4))
            load_e(0)
            load_a(0)
            load_e(1)
            load_y(0)
            for s in range(1, 4):
                load_a(s)
                load_y(s)
            GP.memset(warm[:], 1.0)
            S.activation(out=warm[:], in_=warm[:], func=ACT.Abs_reciprocal_sqrt)
            GP.tensor_copy(out=rho_f[:], in_=rho4[:])
            GP.tensor_scalar(out=rho_2[:], in0=rho4[:], scalar1=2.0, scalar2=0.0, op0=ALU.mult, op1=ALU.add)
            GP.tensor_tensor(out=rho_s[:], in0=rho4[:], in1=rho4[:], op=ALU.mult)
            GP.tensor_scalar(out=rho_h[:], in0=rho_s[:], scalar1=0.5, scalar2=0.0, op0=ALU.mult, op1=ALU.add)

            e1_part(SC, 0, 80, 128)
            b_spread()
            e1_part(VC, 0, 0, 80)
            e2_turn(0, 0)
            a_turn(0, 0)
            e1_quant(0)
            a_turn(0, 1)
            a_mul(0, 0)
            e2_turn(0, 1)
            e1_part(VC, 1, 0, 80)
            a_mul(0, 1)
            e2_copy(0, 0)
            e1_part(SC, 1, 80, 128)
            e1_quant(1)
            a_quant(0)
            a_square(0, 0)
            e2_copy(0, 1)
            e2_quant(0)
            a_rsqrt(0, 0)
            a_square(0, 1)
            y_turn(0)
            y_gain(0, 0)
            mm1(0)
            y_gain(0, 1)
            y_gain(0, 2)
            a_turn(1, 0)
            a_rsqrt(0, 1)
            a_pen(0, 0)
            q_u(0, 0)
            q_u(0, 1)
            e2_turn(1, 0)
            q_x(0, 0)
            a_square(1, 0)
            q_u(0, 2)
            q_u(0, 3)
            q_d(0, 0)
            y_gain(0, 3)
            a_rsqrt(1, 0)
            q_x(0, 2)
            a_pen(0, 1)
            q_slope(0, 0)
            q_d(0, 1)
            e2_copy(1, 0)
            q_d(0, 2)
            q_slope(0, 1)
            e2_turn(1, 1)
            a_turn(1, 1)
            q_d(0, 3)
            a_square(1, 1)
            a_mul(1, 0)
            e2_copy(1, 1)
            a_turn(2, 0)
            a_pen(1, 0)
            q_q(0, 0)
            a_rsqrt(1, 1)
            a_mul(1, 1)
            q_quant(0)
            a_quant(1)
            y_turn(1)
            mm2(0, 0, 0)
            mm2(0, 0, 1)
            a_pen(1, 1)
            e2_quant(1)
            mm2(0, 0, 2)
            a_turn(2, 1)
            mm2(0, 0, 3)
            mm2(0, 1, 0)
            a_square(2, 0)
            mm2(0, 1, 1)
            a_rsqrt(2, 0)
            r_add(0, 0, 0)
            a_mul(2, 0)
            y_gain(1, 0)
            r_add(0, 0, 1)
            mm2(0, 1, 2)
            a_mul(2, 1)
            a_pen(2, 0)
            a_quant(2)
            r_add(0, 0, 2)
            a_square(2, 1)
            mm2(0, 1, 3)
            mm1(1)
            r_add(0, 0, 3)
            a_rsqrt(2, 1)
            o_turn(0, 0, 0)
            r_add(0, 1, 0)
            r_add(0, 1, 1)
            q_u(1, 0)
            y_gain(1, 1)
            r_add(0, 1, 2)
            r_add(0, 1, 3)
            a_pen(2, 1)
            q_x(1, 0)
            q_u(1, 1)
            o_turn(0, 0, 1)
            y_gain(1, 2)
            y_gain(1, 3)
            a_turn(3, 0)
            q_u(1, 2)
            o_turn(0, 1, 0)
            q_x(1, 1)
            p_cast(SC, 0, 0)
            o_copy(SC, 0, 0, 0)
            q_u(1, 3)
            q_x(1, 2)
            o_turn(0, 1, 1)
            a_turn(3, 1)
            q_d(1, 0)
            q_x(1, 3)
            q_d(1, 1)
            o_copy(SC, 0, 0, 1)
            q_slope(1, 0)
            q_d(1, 2)
            y_turn(2)
            a_mul(3, 0)
            a_mul(3, 1)
            o_copy(SC, 0, 1, 0)
            q_slope(1, 1)
            q_d(1, 3)
            o_store(0, 0, 0, L)
            a_quant(3)
            o_copy(SC, 0, 1, 1)
            q_q(1, 0)
            q_q(1, 1)
            mm1(2)
            q_u(2, 0)
            q_u(2, 1)
            q_quant(1)
            q_u(2, 2)
            q_u(2, 3)
            q_x(2, 0)
            a_square(3, 0)
            mm2(1, 0, 0)
            p_cast(SC, 0, 1)
            q_x(2, 2)
            r_add(1, 0, 0)
            mm2(1, 0, 1)
            y_gain(2, 0)
            y_gain(2, 1)
            mm2(1, 0, 2)
            mm2(1, 0, 3)
            r_add(1, 0, 1)
            y_gain(2, 2)
            a_rsqrt(3, 0)
            r_add(1, 0, 2)
            mm2(1, 1, 0)
            mm2(1, 1, 1)
            y_gain(2, 3)
            mm2(1, 1, 2)
            o_store(0, 1, 0, L)
            mm2(1, 1, 3)
            r_add(1, 0, 3)
            r_add(1, 1, 0)
            q_d(2, 0)
            q_slope(2, 0)
            o_turn(1, 0, 0)
            a_square(3, 1)
            q_slope(2, 1)
            q_d(2, 1)
            r_add(1, 1, 1)
            q_d(2, 2)
            a_rsqrt(3, 1)
            o_copy(SC, 1, 0, 0)
            r_add(1, 1, 2)
            o_turn(1, 0, 1)
            q_d(2, 3)
            r_add(1, 1, 3)
            p_cast(VC, 1, 0)
            o_turn(1, 0, 2)
            o_turn(1, 0, 3)
            p_quant(0, 0)
            o_copy(SC, 1, 0, 1)
            q_q(2, 0)
            o_copy(SC, 1, 0, 2)
            a_pen(3, 0)
            o_turn(1, 1, 0)
            o_turn(1, 1, 1)
            o_turn(1, 1, 2)
            o_turn(1, 1, 3)
            o_copy(SC, 1, 0, 3)
            q_quant(2)
            o_copy(SC, 1, 1, 0)
            mm2(2, 0, 0)
            o_store(1, 0, 0, L)
            mm2(2, 0, 1)
            o_copy(SC, 1, 1, 1)
            o_copy(SC, 1, 1, 2)
            o_store(1, 1, 0, L)
            a_pen(3, 1)
            mm2(2, 0, 2)
            o_copy(SC, 1, 1, 3)
            o_store(1, 2, 0, L)
            mm2(2, 0, 3)
            o_store(1, 3, 0, L)
            r_add(2, 0, 0)
            mm2(2, 1, 0)
            p_quant(0, 1)
            p_cast(SC, 1, 1)
            r_add(2, 0, 1)
            mm2(2, 1, 1)
            r_add(2, 0, 2)
            r_add(2, 0, 3)
            p_quant(1, 0)
            mm2(2, 1, 2)
            mm2(2, 1, 3)
            p_quant(1, 1)
            o_turn(2, 0, 0)
            p_cast(SC, 2, 0)
            r_add(2, 1, 0)
            o_copy(SC, 2, 0, 0)
            r_add(2, 1, 1)
            o_turn(2, 0, 1)
            o_copy(SC, 2, 0, 1)
            r_add(2, 1, 2)
            o_store(2, 0, 0, 512)
            store_scales(0, 768)
            r_add(2, 1, 3)
            o_store(2, 1, 0, 512)
            o_turn(2, 1, 0)
            o_turn(2, 1, 1)
            o_copy(SC, 2, 1, 0)
            o_copy(SC, 2, 1, 1)
            p_quant(2, 0)
            p_cast(VC, 2, 1)
            o_store(2, 0, 512, L)
            p_quant(2, 1)
            o_store(2, 1, 512, L)
            store_scales(768, N)
